import numpy as np
import ml_dtypes


def mxq(x, axis, fmt="e4m3"):
    dtype, down = {"e4m3": (ml_dtypes.float8_e4m3fn, 7), "e5m2": (ml_dtypes.float8_e5m2, 14)}[fmt]
    v = np.moveaxis(np.asarray(x, np.float32).astype(ml_dtypes.bfloat16).astype(np.float64), axis, -1)
    blocks = v.reshape(v.shape[:-1] + (-1, 32))
    amax = np.abs(blocks).max(-1, keepdims=True)
    byte = np.maximum(np.where(amax > 0, np.frexp(amax)[1] - 1 + 127, 0) - down, 1)
    scale = np.exp2(byte - 127.0)
    codes = (blocks / scale).astype(np.float32).astype(dtype).astype(np.float64)
    return np.moveaxis((codes * scale).reshape(v.shape), -1, axis)


WIDE = False


def mx_kscale(k):
    if not WIDE:
        return np.ones(k)
    levels = np.array([30, -30])
    if k % 512:
        return np.exp2(np.random.permutation(np.resize(levels, k // 32))).repeat(32)
    a = np.empty((k // 512, 16))
    for p in range(k // 512):
        a[p, :8] = np.random.permutation(np.resize(levels, 8))
        for g in range(8):
            far = levels[np.abs(levels - a[p, g]) >= 10]
            a[p, g + 8] = far[np.random.randint(len(far))]
    return np.exp2(a.ravel()).repeat(32)


def f64(x):
    return np.asarray(x).astype(np.float64)


K, M, T = 1536, 512, 512


def setup_inputs():
    n = np.random.standard_normal
    s1 = mx_kscale(K)[:, None]
    s2 = mx_kscale(K)[:, None]
    return {
        "w": (n((K, M)) / np.sqrt(K) * s1).astype(np.float32),
        "xd": (n((K, T)) / s1).astype(np.float32),
        "wd": (n((K, M)) / np.sqrt(K) * s2).astype(np.float32),
        "x": (n((K, T)) / s2).astype(np.float32),
        "g": (n((512, 512))).astype(np.float32),
    }


def reference(w, xd, wd, x, g):
    w_ = mxq(f64(w), 0, "e4m3")
    xd_ = mxq(f64(xd), 0, "e5m2")
    wd_ = mxq(f64(wd), 0, "e5m2")
    x_ = mxq(f64(x), 0, "e4m3")
    y = xd_.T @ w_ + x_.T @ wd_
    return f64(g) * y

@@ -1,0 +1,143 @@
+from contextlib import ExitStack
+
+import concourse.mybir as mybir
+
+K, M, T = 1536, 512, 512
+
+FLOPS = 2 * 2 * K * M * T
+
+F32 = mybir.dt.float32
+BF16 = mybir.dt.bfloat16
+U32 = mybir.dt.uint32
+U8 = mybir.dt.uint8
+E4M3 = mybir.dt.float8_e4m3fn_x4
+E5M2 = mybir.dt.float8_e5m2_x4
+
+P = 128
+PACK = 4
+K_PASS = P * PACK
+PASSES = K // K_PASS
+TILES = T // P
+HALF = T // 2
+
+
+def round_and_interleave(copy, grp, raw, c0, c1, j0=0):
+    dst = grp[:, PACK * c0 : PACK * c1].rearrange("p (c i j) -> p c j i", i=4, j=PACK)
+    copy(
+        out=dst[:, :, j0 : j0 + raw.shape[1], :],
+        in_=raw[:, :, c0:c1].rearrange("p j (c i) -> p c j i", i=4),
+    )
+
+
+def tile_mix_jvp_tm_mul_kernel(tc, w, xd, wd, x, g, out):
+    nc = tc.nc
+
+    with ExitStack() as ctx:
+        raws = ctx.enter_context(tc.tile_pool(name="raws", bufs=1))
+        stage = ctx.enter_context(tc.tile_pool(name="stage", bufs=4))
+        keep = ctx.enter_context(tc.tile_pool(name="keep", bufs=1))
+        psum = ctx.enter_context(tc.psum_pool(name="psum", bufs=1))
+        ctx.enter_context(tc.manual_schedule())
+
+        def load(name, src, c, c0, c1):
+            r = raws.tile([P, PACK, c1 - c0], F32, name="raw_%s%d_%d" % (name, c, c0), align_bytes=64)
+            rows = src[c * K_PASS : (c + 1) * K_PASS, c0:c1]
+            nc.sync.dma_start(out=r[:], in_=rows.rearrange("(p j) w -> p j w", j=PACK))
+            return r
+
+        raw = {}
+        for name, src in (("w", w), ("wd", wd), ("xd", xd)):
+            for c in range(PASSES):
+                raw[name, c] = load(name, src, c, 0, T)
+        raw["x", 0] = load("x", x, 0, 0, T)
+        raw_x2a = load("x", x, 2, 0, HALF)
+        raw_x1 = []
+        rows = x[K_PASS : 2 * K_PASS, :].rearrange("(p j) w -> p j w", j=PACK)
+        for h in range(2):
+            r = raws.tile([P, 2, T], F32, name="raw_x1_%d" % h, align_bytes=64)
+            nc.sync.dma_start(out=r[:], in_=rows[:, 2 * h : 2 * h + 2, :])
+            raw_x1.append(r)
+        raw_x2b = load("x", x, 2, HALF, T)
+        gs = []
+        for i in range(TILES):
+            gt = keep.tile([P, M], F32, name="g%d" % i, align_bytes=64)
+            nc.sync.dma_start(out=gt[:], in_=g[i * P : (i + 1) * P, :])
+            gs.append(gt)
+
+        acc = [psum.tile([P, M], F32, name="acc%d" % i) for i in range(TILES)]
+
+        def quantise(name, grp, c0, c1, fmt):
+            width = c1 - c0
+            cd = keep.tile([P, width], U32, name="codes_%s" % name, align_bytes=64)
+            sc = keep.tile([P, width], U8, name="scales_%s" % name, align_bytes=64)
+            nc.vector.quantize_mx(out=cd[:].bitcast(fmt), scales=sc[:], in_=grp[:, PACK * c0 : PACK * c1])
+            return cd, sc
+
+        moving = {}
+
+        def multiply(name, c, i, operand, c0, start=False, stop=False):
+            wname, lfmt, rfmt = ("w", E5M2, E4M3) if name == "xd" else ("wd", E4M3, E5M2)
+            cols = slice(i * P - c0, (i + 1) * P - c0)
+            nc.tensor.matmul_mx(
+                out=acc[i][:],
+                lhsT=operand[0][:, cols].bitcast(lfmt),
+                lhsT_scale=operand[1][:, cols],
+                rhs=moving[wname, c][0][:].bitcast(rfmt),
+                rhs_scale=moving[wname, c][1][:],
+                start=start,
+                stop=stop,
+            )
+
+        for name, fmt in (("w", E4M3), ("wd", E5M2), ("xd", E5M2), ("x", E4M3)):
+            for c in range(1 if name == "x" else PASSES):
+                grp = stage.tile([P, PACK * T], BF16, name="grp", align_bytes=64)
+                round_and_interleave(nc.vector.tensor_copy, grp, raw[name, c], 0, HALF)
+                round_and_interleave(nc.scalar.copy, grp, raw[name, c], HALF, T)
+                operand = quantise("%s%d" % (name, c), grp, 0, T, fmt)
+                if name in ("w", "wd"):
+                    moving[name, c] = operand
+                else:
+                    for i in range(TILES):
+                        multiply(name, c, i, operand, 0, start=(name == "xd" and c == 0))
+
+        grp = stage.tile([P, PACK * HALF], BF16, name="grp_x2a", align_bytes=64)
+        round_and_interleave(nc.vector.tensor_copy, grp, raw_x2a, 0, P)
+        round_and_interleave(nc.scalar.copy, grp, raw_x2a, P, HALF)
+        operand = quantise("x2a", grp, 0, HALF, E4M3)
+        for i in (0, 1):
+            multiply("x", 2, i, operand, 0)
+
+        grp = stage.tile([P, PACK * T], BF16, name="grp", align_bytes=64)
+        for h in range(2):
+            round_and_interleave(nc.vector.tensor_copy, grp, raw_x1[h], 0, HALF, 2 * h)
+            round_and_interleave(nc.scalar.copy, grp, raw_x1[h], HALF, T, 2 * h)
+        for i in (0, 1):
+            operand = quantise("x1_%d" % i, grp, i * P, (i + 1) * P, E4M3)
+            multiply("x", 1, i, operand, i * P, stop=True)
+        operand = quantise("x1b", grp, HALF, T, E4M3)
+        for i in (2, 3):
+            multiply("x", 1, i, operand, HALF)
+
+        grp_x2b = stage.tile([P, PACK * HALF], BF16, name="grp_x2b", align_bytes=64)
+        round_and_interleave(nc.scalar.copy, grp_x2b, raw_x2b, 0, P)
+        round_and_interleave(nc.scalar.copy, grp_x2b, raw_x2b, P + 64, HALF)
+        round_and_interleave(nc.vector.tensor_copy, grp_x2b, raw_x2b, P, P + 64)
+
+        def last_product(i):
+            operand = quantise("x2b%d" % i, grp_x2b, (i - 2) * P, (i - 1) * P, E4M3)
+            multiply("x", 2, i, operand, i * P, stop=True)
+
+        def finish(i, pieces):
+            width = M // pieces
+            for h in range(pieces):
+                cols = slice(h * width, (h + 1) * width)
+                res = keep.tile([P, width], F32, name="res%d_%d" % (i, h), align_bytes=64)
+                nc.vector.tensor_mul(out=res[:], in0=acc[i][:, cols], in1=gs[i][:, cols])
+                nc.sync.dma_start(out=out[i * P : (i + 1) * P, cols], in_=res[:])
+
+        last_product(2)
+        finish(0, 2)
+        last_product(3)
+        finish(1, 1)
+        finish(2, 1)
+        finish(3, 2)

@@ -46,9 +46,21 @@ def tile_mix_jvp_tm_mul_kernel(tc, w, xd, wd, x, g, out):
             return r
 
         raw = {}
-        for name, src in (("w", w), ("wd", wd), ("xd", xd)):
-            for c in range(PASSES):
-                raw[name, c] = load(name, src, c, 0, T)
+
+        def load_passes(name, src, first, count):
+            r = raws.tile([P, count, PACK, T], F32, name="raw_%s%d" % (name, first), align_bytes=64)
+            rows = src[first * K_PASS : (first + count) * K_PASS, :]
+            nc.sync.dma_start(
+                out=r[:].rearrange("p c j w -> p c (j w)"),
+                in_=rows.rearrange("(c p j) w -> p c (j w)", p=P, j=PACK),
+            )
+            for c in range(count):
+                raw[name, first + c] = r[:, c, :, :]
+
+        load_passes("w", w, 0, PASSES)
+        load_passes("wd", wd, 0, PASSES)
+        load_passes("xd", xd, 0, PASSES - 1)
+        load_passes("xd", xd, PASSES - 1, 1)
         raw["x", 0] = load("x", x, 0, 0, T)
         raw_x2a = load("x", x, 2, 0, HALF)
         raw_x1 = []

@@ -21,12 +21,9 @@ TILES = T // P
 HALF = T // 2
 
 
-def round_and_interleave(copy, grp, raw, c0, c1, j0=0):
+def round_and_interleave(copy, grp, raw, c0, c1):
     dst = grp[:, PACK * c0 : PACK * c1].rearrange("p (c i j) -> p c j i", i=4, j=PACK)
-    copy(
-        out=dst[:, :, j0 : j0 + raw.shape[1], :],
-        in_=raw[:, :, c0:c1].rearrange("p j (c i) -> p c j i", i=4),
-    )
+    copy(out=dst, in_=raw[:, :, c0:c1].rearrange("p j (c i) -> p c j i", i=4))
 
 
 def tile_mix_jvp_tm_mul_kernel(tc, w, xd, wd, x, g, out):
@@ -34,18 +31,9 @@ def tile_mix_jvp_tm_mul_kernel(tc, w, xd, wd, x, g, out):
 
     with ExitStack() as ctx:
         raws = ctx.enter_context(tc.tile_pool(name="raws", bufs=1))
-        stage = ctx.enter_context(tc.tile_pool(name="stage", bufs=4))
         keep = ctx.enter_context(tc.tile_pool(name="keep", bufs=1))
         psum = ctx.enter_context(tc.psum_pool(name="psum", bufs=1))
         ctx.enter_context(tc.manual_schedule())
-
-        def load(name, src, c, c0, c1):
-            r = raws.tile([P, PACK, c1 - c0], F32, name="raw_%s%d_%d" % (name, c, c0), align_bytes=64)
-            rows = src[c * K_PASS : (c + 1) * K_PASS, c0:c1]
-            nc.sync.dma_start(out=r[:], in_=rows.rearrange("(p j) w -> p j w", j=PACK))
-            return r
-
-        raw = {}
 
         def load_passes(name, src, first, count):
             r = raws.tile([P, count, PACK, T], F32, name="raw_%s%d" % (name, first), align_bytes=64)
@@ -54,27 +42,22 @@ def tile_mix_jvp_tm_mul_kernel(tc, w, xd, wd, x, g, out):
                 out=r[:].rearrange("p c j w -> p c (j w)"),
                 in_=rows.rearrange("(c p j) w -> p c (j w)", p=P, j=PACK),
             )
-            for c in range(count):
-                raw[name, first + c] = r[:, c, :, :]
+            return [r[:, c, :, :] for c in range(count)]
 
-        load_passes("w", w, 0, PASSES)
-        load_passes("wd", wd, 0, PASSES)
-        load_passes("xd", xd, 0, PASSES - 1)
-        load_passes("xd", xd, PASSES - 1, 1)
-        raw["x", 0] = load("x", x, 0, 0, T)
-        raw_x2a = load("x", x, 2, 0, HALF)
-        raw_x1 = []
-        rows = x[K_PASS : 2 * K_PASS, :].rearrange("(p j) w -> p j w", j=PACK)
-        for h in range(2):
-            r = raws.tile([P, 2, T], F32, name="raw_x1_%d" % h, align_bytes=64)
-            nc.sync.dma_start(out=r[:], in_=rows[:, 2 * h : 2 * h + 2, :])
-            raw_x1.append(r)
-        raw_x2b = load("x", x, 2, HALF, T)
-        gs = []
-        for i in range(TILES):
-            gt = keep.tile([P, M], F32, name="g%d" % i, align_bytes=64)
-            nc.sync.dma_start(out=gt[:], in_=g[i * P : (i + 1) * P, :])
-            gs.append(gt)
+        def load_columns(name, src, c, c0, c1):
+            r = raws.tile([P, PACK, c1 - c0], F32, name="raw_%s%d_%d" % (name, c, c0), align_bytes=64)
+            rows = src[c * K_PASS : (c + 1) * K_PASS, c0:c1]
+            nc.sync.dma_start(out=r[:], in_=rows.rearrange("(p j) w -> p j w", j=PACK))
+            return r[:]
+
+        def load_g(first, count):
+            gt = keep.tile([P, count, M], F32, name="g%d" % first, align_bytes=64)
+            rows = g[first * P : (first + count) * P, :]
+            nc.sync.dma_start(out=gt[:], in_=rows.rearrange("(i p) n -> p i n", p=P))
+            return [gt[:, i, :] for i in range(count)]
+
+        def grouped(name, width):
+            return keep.tile([P, PACK * width], BF16, name="grp_%s" % name, align_bytes=64)
 
         acc = [psum.tile([P, M], F32, name="acc%d" % i) for i in range(TILES)]
 
@@ -100,56 +83,85 @@ def tile_mix_jvp_tm_mul_kernel(tc, w, xd, wd, x, g, out):
                 stop=stop,
             )
 
-        for name, fmt in (("w", E4M3), ("wd", E5M2), ("xd", E5M2), ("x", E4M3)):
-            for c in range(1 if name == "x" else PASSES):
-                grp = stage.tile([P, PACK * T], BF16, name="grp", align_bytes=64)
-                round_and_interleave(nc.vector.tensor_copy, grp, raw[name, c], 0, HALF)
-                round_and_interleave(nc.scalar.copy, grp, raw[name, c], HALF, T)
-                operand = quantise("%s%d" % (name, c), grp, 0, T, fmt)
+        def whole_passes(name, fmt, first, raw, split=HALF):
+            grps = []
+
+            def copy(n):
+                grp = grouped("%s%d" % (name, first + n), T)
+                round_and_interleave(nc.vector.tensor_copy, grp, raw[n], 0, split)
+                round_and_interleave(nc.scalar.copy, grp, raw[n], split, T)
+                grps.append(grp)
+
+            copy(0)
+            for n in range(len(raw)):
+                if n + 1 < len(raw):
+                    copy(n + 1)
+                c = first + n
+                operand = quantise("%s%d" % (name, c), grps[n], 0, T, fmt)
                 if name in ("w", "wd"):
                     moving[name, c] = operand
                 else:
                     for i in range(TILES):
                         multiply(name, c, i, operand, 0, start=(name == "xd" and c == 0))
 
-        grp = stage.tile([P, PACK * HALF], BF16, name="grp_x2a", align_bytes=64)
-        round_and_interleave(nc.vector.tensor_copy, grp, raw_x2a, 0, P)
-        round_and_interleave(nc.scalar.copy, grp, raw_x2a, P, HALF)
-        operand = quantise("x2a", grp, 0, HALF, E4M3)
+        res = [keep.tile([P, M], F32, name="res%d" % i, align_bytes=64) for i in range(TILES)]
+
+        def scale(i, c0, c1):
+            nc.vector.tensor_mul(out=res[i][:, c0:c1], in0=acc[i][:, c0:c1], in1=gs[i][:, c0:c1])
+
+        def store(i, c0, c1):
+            nc.sync.dma_start(out=out[i * P : (i + 1) * P, c0:c1], in_=res[i][:, c0:c1])
+
+        raw_w = load_passes("w", w, 0, 3)
+        raw_wd = load_passes("wd", wd, 0, 3)
+        raw_xd01 = load_passes("xd", xd, 0, 2)
+        raw_xd2 = load_passes("xd", xd, 2, 1)
+        raw_x0 = load_passes("x", x, 0, 1)
+        raw_x1 = load_passes("x", x, 1, 1)[0]
+        raw_x2l = load_columns("x", x, 2, 0, HALF)
+        gs = load_g(0, 2)
+        raw_t2 = load_columns("x", x, 2, HALF, HALF + P)
+        raw_t3 = load_columns("x", x, 2, HALF + P, T)
+        gs = gs + load_g(2, 1) + load_g(3, 1)
+
+        whole_passes("w", E4M3, 0, raw_w)
+        whole_passes("wd", E5M2, 0, raw_wd)
+        whole_passes("xd", E5M2, 0, raw_xd01)
+        whole_passes("xd", E5M2, 2, raw_xd2)
+        whole_passes("x", E4M3, 0, raw_x0)
+
+        V, S = nc.vector.tensor_copy, nc.scalar.copy
+        grp_x1 = grouped("x1", T)
+        round_and_interleave(V, grp_x1, raw_x1, 0, 160)
+        round_and_interleave(S, grp_x1, raw_x1, 160, HALF)
+        round_and_interleave(V, grp_x1, raw_x1, HALF, HALF + P)
+        round_and_interleave(S, grp_x1, raw_x1, HALF + P, T)
+        operand = quantise("x1l", grp_x1, 0, HALF, E4M3)
         for i in (0, 1):
-            multiply("x", 2, i, operand, 0)
+            multiply("x", 1, i, operand, 0)
 
-        grp = stage.tile([P, PACK * T], BF16, name="grp", align_bytes=64)
-        for h in range(2):
-            round_and_interleave(nc.vector.tensor_copy, grp, raw_x1[h], 0, HALF, 2 * h)
-            round_and_interleave(nc.scalar.copy, grp, raw_x1[h], HALF, T, 2 * h)
+        grp_x2l = grouped("x2l", HALF)
+        round_and_interleave(V, grp_x2l, raw_x2l, 0, P)
+        round_and_interleave(S, grp_x2l, raw_x2l, P, HALF)
+        x1r = quantise("x1r", grp_x1, HALF, T, E4M3)
         for i in (0, 1):
-            operand = quantise("x1_%d" % i, grp, i * P, (i + 1) * P, E4M3)
-            multiply("x", 1, i, operand, i * P, stop=True)
-        operand = quantise("x1b", grp, HALF, T, E4M3)
-        for i in (2, 3):
-            multiply("x", 1, i, operand, HALF)
-
-        grp_x2b = stage.tile([P, PACK * HALF], BF16, name="grp_x2b", align_bytes=64)
-        round_and_interleave(nc.scalar.copy, grp_x2b, raw_x2b, 0, P)
-        round_and_interleave(nc.scalar.copy, grp_x2b, raw_x2b, P + 64, HALF)
-        round_and_interleave(nc.vector.tensor_copy, grp_x2b, raw_x2b, P, P + 64)
-
-        def last_product(i):
-            operand = quantise("x2b%d" % i, grp_x2b, (i - 2) * P, (i - 1) * P, E4M3)
+            operand = quantise("x2_%d" % i, grp_x2l, i * P, (i + 1) * P, E4M3)
             multiply("x", 2, i, operand, i * P, stop=True)
+        for i in (2, 3):
+            multiply("x", 1, i, x1r, HALF)
 
-        def finish(i, pieces):
-            width = M // pieces
-            for h in range(pieces):
-                cols = slice(h * width, (h + 1) * width)
-                res = keep.tile([P, width], F32, name="res%d_%d" % (i, h), align_bytes=64)
-                nc.vector.tensor_mul(out=res[:], in0=acc[i][:, cols], in1=gs[i][:, cols])
-                nc.sync.dma_start(out=out[i * P : (i + 1) * P, cols], in_=res[:])
-
-        last_product(2)
-        finish(0, 2)
-        last_product(3)
-        finish(1, 1)
-        finish(2, 1)
-        finish(3, 2)
+        grp_t2 = grouped("t2", P)
+        grp_t3 = grouped("t3", P)
+        round_and_interleave(S, grp_t2, raw_t2, 0, P)
+        round_and_interleave(S, grp_t3, raw_t3, 0, P)
+        scale(0, 0, M)
+        store(0, 0, M)
+        scale(1, 0, HALF)
+        multiply("x", 2, 2, quantise("x2_2", grp_t2, 0, P, E4M3), 2 * P, stop=True)
+        scale(1, HALF, M)
+        store(1, 0, M)
+        multiply("x", 2, 3, quantise("x2_3", grp_t3, 0, P, E4M3), 3 * P, stop=True)
+        for i in (2, 3):
+            for c0 in (0, HALF):
+                scale(i, c0, c0 + HALF)
+                store(i, c0, c0 + HALF)

@@ -21,9 +21,9 @@ TILES = T // P
 HALF = T // 2
 
 
-def round_and_interleave(copy, grp, raw, c0, c1):
+def round_and_interleave(copy, grp, raw, c0, c1, j0=0):
     dst = grp[:, PACK * c0 : PACK * c1].rearrange("p (c i j) -> p c j i", i=4, j=PACK)
-    copy(out=dst, in_=raw[:, :, c0:c1].rearrange("p j (c i) -> p c j i", i=4))
+    copy(out=dst[:, :, j0 : j0 + raw.shape[1], :], in_=raw[:, :, c0:c1].rearrange("p j (c i) -> p c j i", i=4))
 
 
 def tile_mix_jvp_tm_mul_kernel(tc, w, xd, wd, x, g, out):
@@ -117,12 +117,17 @@ def tile_mix_jvp_tm_mul_kernel(tc, w, xd, wd, x, g, out):
         raw_xd01 = load_passes("xd", xd, 0, 2)
         raw_xd2 = load_passes("xd", xd, 2, 1)
         raw_x0 = load_passes("x", x, 0, 1)
-        raw_x1 = load_passes("x", x, 1, 1)[0]
-        raw_x2l = load_columns("x", x, 2, 0, HALF)
-        gs = load_g(0, 2)
-        raw_t2 = load_columns("x", x, 2, HALF, HALF + P)
-        raw_t3 = load_columns("x", x, 2, HALF + P, T)
-        gs = gs + load_g(2, 1) + load_g(3, 1)
+        raw_x2a = load_columns("x", x, 2, 0, HALF)
+        raw_x1 = []
+        rows = x[K_PASS : 2 * K_PASS, :].rearrange("(p j) w -> p j w", j=PACK)
+        for h in range(2):
+            r = raws.tile([P, 2, T], F32, name="raw_x1_%d" % h, align_bytes=64)
+            nc.sync.dma_start(out=r[:], in_=rows[:, 2 * h : 2 * h + 2, :])
+            raw_x1.append(r)
+        raw_x2b = load_columns("x", x, 2, HALF, T)
+        gs = []
+        for i in range(TILES):
+            gs.extend(load_g(i, 1))
 
         whole_passes("w", E4M3, 0, raw_w)
         whole_passes("wd", E5M2, 0, raw_wd)
@@ -131,37 +136,42 @@ def tile_mix_jvp_tm_mul_kernel(tc, w, xd, wd, x, g, out):
         whole_passes("x", E4M3, 0, raw_x0)
 
         V, S = nc.vector.tensor_copy, nc.scalar.copy
-        grp_x1 = grouped("x1", T)
-        round_and_interleave(V, grp_x1, raw_x1, 0, 160)
-        round_and_interleave(S, grp_x1, raw_x1, 160, HALF)
-        round_and_interleave(V, grp_x1, raw_x1, HALF, HALF + P)
-        round_and_interleave(S, grp_x1, raw_x1, HALF + P, T)
-        operand = quantise("x1l", grp_x1, 0, HALF, E4M3)
+        grp = grouped("x2a", HALF)
+        round_and_interleave(V, grp, raw_x2a, 0, P)
+        round_and_interleave(S, grp, raw_x2a, P, HALF)
+        operand = quantise("x2a", grp, 0, HALF, E4M3)
         for i in (0, 1):
-            multiply("x", 1, i, operand, 0)
+            multiply("x", 2, i, operand, 0)
 
-        grp_x2l = grouped("x2l", HALF)
-        round_and_interleave(V, grp_x2l, raw_x2l, 0, P)
-        round_and_interleave(S, grp_x2l, raw_x2l, P, HALF)
-        x1r = quantise("x1r", grp_x1, HALF, T, E4M3)
+        grp = grouped("x1", T)
+        for h in range(2):
+            round_and_interleave(V, grp, raw_x1[h], 0, HALF, 2 * h)
+            round_and_interleave(S, grp, raw_x1[h], HALF, T, 2 * h)
         for i in (0, 1):
-            operand = quantise("x2_%d" % i, grp_x2l, i * P, (i + 1) * P, E4M3)
+            operand = quantise("x1_%d" % i, grp, i * P, (i + 1) * P, E4M3)
+            multiply("x", 1, i, operand, i * P, stop=True)
+        operand = quantise("x1b", grp, HALF, T, E4M3)
+        for i in (2, 3):
+            multiply("x", 1, i, operand, HALF)
+
+        grp_x2b = grouped("x2b", HALF)
+        round_and_interleave(S, grp_x2b, raw_x2b, 0, P)
+        round_and_interleave(S, grp_x2b, raw_x2b, P + 64, HALF)
+        round_and_interleave(V, grp_x2b, raw_x2b, P, P + 64)
+
+        def last_product(i):
+            operand = quantise("x2b%d" % i, grp_x2b, (i - 2) * P, (i - 1) * P, E4M3)
             multiply("x", 2, i, operand, i * P, stop=True)
-        for i in (2, 3):
-            multiply("x", 1, i, x1r, HALF)
 
-        grp_t2 = grouped("t2", P)
-        grp_t3 = grouped("t3", P)
-        round_and_interleave(S, grp_t2, raw_t2, 0, P)
-        round_and_interleave(S, grp_t3, raw_t3, 0, P)
-        scale(0, 0, M)
-        store(0, 0, M)
-        scale(1, 0, HALF)
-        multiply("x", 2, 2, quantise("x2_2", grp_t2, 0, P, E4M3), 2 * P, stop=True)
-        scale(1, HALF, M)
-        store(1, 0, M)
-        multiply("x", 2, 3, quantise("x2_3", grp_t3, 0, P, E4M3), 3 * P, stop=True)
-        for i in (2, 3):
-            for c0 in (0, HALF):
-                scale(i, c0, c0 + HALF)
-                store(i, c0, c0 + HALF)
+        def finish(i, pieces):
+            width = M // pieces
+            for h in range(pieces):
+                scale(i, h * width, (h + 1) * width)
+                store(i, h * width, (h + 1) * width)
+
+        last_product(2)
+        finish(0, 2)
+        last_product(3)
+        finish(1, 1)
+        finish(2, 1)
+        finish(3, 2)

@@ -117,61 +117,59 @@ def tile_mix_jvp_tm_mul_kernel(tc, w, xd, wd, x, g, out):
         raw_xd01 = load_passes("xd", xd, 0, 2)
         raw_xd2 = load_passes("xd", xd, 2, 1)
         raw_x0 = load_passes("x", x, 0, 1)
-        raw_x2a = load_columns("x", x, 2, 0, HALF)
-        raw_x1 = []
-        rows = x[K_PASS : 2 * K_PASS, :].rearrange("(p j) w -> p j w", j=PACK)
-        for h in range(2):
-            r = raws.tile([P, 2, T], F32, name="raw_x1_%d" % h, align_bytes=64)
-            nc.sync.dma_start(out=r[:], in_=rows[:, 2 * h : 2 * h + 2, :])
-            raw_x1.append(r)
-        raw_x2b = load_columns("x", x, 2, HALF, T)
         gs = []
-        for i in range(TILES):
-            gs.extend(load_g(i, 1))
+        raw_x2L = load_columns("x", x, 2, 0, HALF)
+        raw_x1L = load_columns("x", x, 1, 0, HALF)
+        raw_x1R = load_columns("x", x, 1, HALF, T)
+        raw_x2R = load_columns("x", x, 2, HALF, T)
+        gs = gs + load_g(0, 1)
+        gs = gs + load_g(1, 1)
+        gs = gs + load_g(2, 1)
+        gs = gs + load_g(3, 1)
 
-        whole_passes("w", E4M3, 0, raw_w)
-        whole_passes("wd", E5M2, 0, raw_wd)
-        whole_passes("xd", E5M2, 0, raw_xd01)
-        whole_passes("xd", E5M2, 2, raw_xd2)
-        whole_passes("x", E4M3, 0, raw_x0)
-
+        whole_passes("w", E4M3, 0, raw_w, 320)
+        whole_passes("wd", E5M2, 0, raw_wd, 320)
+        whole_passes("xd", E5M2, 0, raw_xd01, 320)
+        whole_passes("xd", E5M2, 2, raw_xd2, 320)
         V, S = nc.vector.tensor_copy, nc.scalar.copy
-        grp = grouped("x2a", HALF)
-        round_and_interleave(V, grp, raw_x2a, 0, P)
-        round_and_interleave(S, grp, raw_x2a, P, HALF)
-        operand = quantise("x2a", grp, 0, HALF, E4M3)
-        for i in (0, 1):
-            multiply("x", 2, i, operand, 0)
 
-        grp = grouped("x1", T)
-        for h in range(2):
-            round_and_interleave(V, grp, raw_x1[h], 0, HALF, 2 * h)
-            round_and_interleave(S, grp, raw_x1[h], HALF, T, 2 * h)
-        for i in (0, 1):
-            operand = quantise("x1_%d" % i, grp, i * P, (i + 1) * P, E4M3)
-            multiply("x", 1, i, operand, i * P, stop=True)
-        operand = quantise("x1b", grp, HALF, T, E4M3)
-        for i in (2, 3):
-            multiply("x", 1, i, operand, HALF)
+        def copy_shared(name, raw, width, c0, c1, share):
+            if name not in grps:
+                grps[name] = grouped(name, width)
+            mid = c0 + share
+            if mid > c0:
+                round_and_interleave(V, grps[name], raw, c0, mid)
+            if mid < c1:
+                round_and_interleave(S, grps[name], raw, mid, c1)
 
-        grp_x2b = grouped("x2b", HALF)
-        round_and_interleave(S, grp_x2b, raw_x2b, 0, P)
-        round_and_interleave(S, grp_x2b, raw_x2b, P + 64, HALF)
-        round_and_interleave(V, grp_x2b, raw_x2b, P, P + 64)
+        def product(name, c, tiles, g0, stop):
+            c0, c1 = tiles[0] * P, (tiles[-1] + 1) * P
+            operand = quantise("%s_%d" % (name, c0), grps[name], c0 - g0, c1 - g0, E4M3)
+            for i in tiles:
+                multiply("x", c, i, operand, c0, stop=stop)
 
-        def last_product(i):
-            operand = quantise("x2b%d" % i, grp_x2b, (i - 2) * P, (i - 1) * P, E4M3)
-            multiply("x", 2, i, operand, i * P, stop=True)
+        def finish(i, c0, c1):
+            scale(i, c0, c1)
+            store(i, c0, c1)
 
-        def finish(i, pieces):
-            width = M // pieces
-            for h in range(pieces):
-                scale(i, h * width, (h + 1) * width)
-                store(i, h * width, (h + 1) * width)
-
-        last_product(2)
-        finish(0, 2)
-        last_product(3)
-        finish(1, 1)
-        finish(2, 1)
-        finish(3, 2)
+        grps = {}
+        copy_shared("x0", raw_x0[0], T, 0, T, 320)
+        copy_shared("x2L", raw_x2L, HALF, 0, HALF, 128)
+        product("x0", 0, (0, 1, 2, 3), 0, False)
+        copy_shared("x1L", raw_x1L, HALF, 0, HALF, 128)
+        product("x2L", 2, (0, 1), 0, False)
+        product("x1L", 1, (0,), 0, True)
+        product("x1L", 1, (1,), 0, True)
+        copy_shared("x1R", raw_x1R, HALF, 0, HALF, 160)
+        product("x1R", 1, (2, 3), HALF, False)
+        copy_shared("x2R", raw_x2R, HALF, 0, HALF, 128)
+        finish(0, 0, HALF)
+        product("x2R", 2, (2,), HALF, True)
+        product("x2R", 2, (3,), HALF, True)
+        finish(0, HALF, M)
+        finish(1, 0, HALF)
+        finish(1, HALF, M)
+        finish(2, 0, HALF)
+        finish(2, HALF, M)
+        finish(3, 0, HALF)
+        finish(3, HALF, M)

@@ -112,25 +112,25 @@ def tile_mix_jvp_tm_mul_kernel(tc, w, xd, wd, x, g, out):
         def store(i, c0, c1):
             nc.sync.dma_start(out=out[i * P : (i + 1) * P, c0:c1], in_=res[i][:, c0:c1])
 
-        raw_w = load_passes("w", w, 0, 3)
-        raw_wd = load_passes("wd", wd, 0, 3)
-        raw_xd01 = load_passes("xd", xd, 0, 2)
-        raw_xd2 = load_passes("xd", xd, 2, 1)
+        raw_w = [load_passes("w", w, c, 1) for c in range(3)]
+        raw_wd = [load_passes("wd", wd, c, 1) for c in range(3)]
+        raw_xd = [load_passes("xd", xd, c, 1) for c in range(3)]
         raw_x0 = load_passes("x", x, 0, 1)
         gs = []
         raw_x2L = load_columns("x", x, 2, 0, HALF)
-        raw_x1L = load_columns("x", x, 1, 0, HALF)
-        raw_x1R = load_columns("x", x, 1, HALF, T)
+        raw_x1 = load_passes("x", x, 1, 1)[0]
         raw_x2R = load_columns("x", x, 2, HALF, T)
         gs = gs + load_g(0, 1)
         gs = gs + load_g(1, 1)
         gs = gs + load_g(2, 1)
         gs = gs + load_g(3, 1)
 
-        whole_passes("w", E4M3, 0, raw_w, 320)
-        whole_passes("wd", E5M2, 0, raw_wd, 320)
-        whole_passes("xd", E5M2, 0, raw_xd01, 320)
-        whole_passes("xd", E5M2, 2, raw_xd2, 320)
+        for c in range(3):
+            whole_passes("w", E4M3, c, raw_w[c], 320)
+        for c in range(3):
+            whole_passes("wd", E5M2, c, raw_wd[c], 320)
+        for c in range(3):
+            whole_passes("xd", E5M2, c, raw_xd[c], 320)
         V, S = nc.vector.tensor_copy, nc.scalar.copy
 
         def copy_shared(name, raw, width, c0, c1, share):
@@ -156,20 +156,16 @@ def tile_mix_jvp_tm_mul_kernel(tc, w, xd, wd, x, g, out):
         copy_shared("x0", raw_x0[0], T, 0, T, 320)
         copy_shared("x2L", raw_x2L, HALF, 0, HALF, 128)
         product("x0", 0, (0, 1, 2, 3), 0, False)
-        copy_shared("x1L", raw_x1L, HALF, 0, HALF, 128)
         product("x2L", 2, (0, 1), 0, False)
-        product("x1L", 1, (0,), 0, True)
-        product("x1L", 1, (1,), 0, True)
-        copy_shared("x1R", raw_x1R, HALF, 0, HALF, 160)
-        product("x1R", 1, (2, 3), HALF, False)
+        copy_shared("x1", raw_x1, T, 0, HALF, 160)
+        copy_shared("x1", raw_x1, T, HALF, T, 128)
+        product("x1", 1, (0,), 0, True)
+        product("x1", 1, (1,), 0, True)
         copy_shared("x2R", raw_x2R, HALF, 0, HALF, 128)
-        finish(0, 0, HALF)
+        product("x1", 1, (2, 3), 0, False)
         product("x2R", 2, (2,), HALF, True)
+        finish(0, 0, M)
         product("x2R", 2, (3,), HALF, True)
-        finish(0, HALF, M)
-        finish(1, 0, HALF)
-        finish(1, HALF, M)
-        finish(2, 0, HALF)
-        finish(2, HALF, M)
-        finish(3, 0, HALF)
-        finish(3, HALF, M)
+        finish(1, 0, M)
+        finish(2, 0, M)
+        finish(3, 0, M)

@@ -36,7 +36,7 @@ def tile_mix_jvp_tm_mul_kernel(tc, w, xd, wd, x, g, out):
         ctx.enter_context(tc.manual_schedule())
 
         def load_passes(name, src, first, count):
-            r = raws.tile([P, count, PACK, T], F32, name="raw_%s%d" % (name, first), align_bytes=64)
+            r = raws.tile([P, count, PACK, T], F32, name="raw_%s%d" % (name, first), align_bytes=256)
             rows = src[first * K_PASS : (first + count) * K_PASS, :]
             nc.sync.dma_start(
                 out=r[:].rearrange("p c j w -> p c (j w)"),
@@ -45,13 +45,13 @@ def tile_mix_jvp_tm_mul_kernel(tc, w, xd, wd, x, g, out):
             return [r[:, c, :, :] for c in range(count)]
 
         def load_columns(name, src, c, c0, c1):
-            r = raws.tile([P, PACK, c1 - c0], F32, name="raw_%s%d_%d" % (name, c, c0), align_bytes=64)
+            r = raws.tile([P, PACK, c1 - c0], F32, name="raw_%s%d_%d" % (name, c, c0), align_bytes=256)
             rows = src[c * K_PASS : (c + 1) * K_PASS, c0:c1]
             nc.sync.dma_start(out=r[:], in_=rows.rearrange("(p j) w -> p j w", j=PACK))
             return r[:]
 
         def load_g(first, count):
-            gt = keep.tile([P, count, M], F32, name="g%d" % first, align_bytes=64)
+            gt = keep.tile([P, count, M], F32, name="g%d" % first, align_bytes=256)
             rows = g[first * P : (first + count) * P, :]
             nc.sync.dma_start(out=gt[:], in_=rows.rearrange("(i p) n -> p i n", p=P))
             return [gt[:, i, :] for i in range(count)]
@@ -104,7 +104,7 @@ def tile_mix_jvp_tm_mul_kernel(tc, w, xd, wd, x, g, out):
                     for i in range(TILES):
                         multiply(name, c, i, operand, 0, start=(name == "xd" and c == 0))
 
-        res = [keep.tile([P, M], F32, name="res%d" % i, align_bytes=64) for i in range(TILES)]
+        res = [keep.tile([P, M], F32, name="res%d" % i, align_bytes=256) for i in range(TILES)]
 
         def scale(i, c0, c1):
             nc.vector.tensor_mul(out=res[i][:, c0:c1], in0=acc[i][:, c0:c1], in1=gs[i][:, c0:c1])

@@ -112,9 +112,10 @@ def tile_mix_jvp_tm_mul_kernel(tc, w, xd, wd, x, g, out):
         def store(i, c0, c1):
             nc.sync.dma_start(out=out[i * P : (i + 1) * P, c0:c1], in_=res[i][:, c0:c1])
 
-        raw_w = [load_passes("w", w, c, 1) for c in range(3)]
-        raw_wd = [load_passes("wd", wd, c, 1) for c in range(3)]
-        raw_xd = [load_passes("xd", xd, c, 1) for c in range(3)]
+        raw_w = load_passes("w", w, 0, 3)
+        raw_wd = load_passes("wd", wd, 0, 3)
+        raw_xd01 = load_passes("xd", xd, 0, 2)
+        raw_xd2 = load_passes("xd", xd, 2, 1)
         raw_x0 = load_passes("x", x, 0, 1)
         gs = []
         raw_x2L = load_columns("x", x, 2, 0, HALF)
@@ -125,12 +126,10 @@ def tile_mix_jvp_tm_mul_kernel(tc, w, xd, wd, x, g, out):
         gs = gs + load_g(2, 1)
         gs = gs + load_g(3, 1)
 
-        for c in range(3):
-            whole_passes("w", E4M3, c, raw_w[c], 320)
-        for c in range(3):
-            whole_passes("wd", E5M2, c, raw_wd[c], 320)
-        for c in range(3):
-            whole_passes("xd", E5M2, c, raw_xd[c], 320)
+        whole_passes("w", E4M3, 0, raw_w, 320)
+        whole_passes("wd", E5M2, 0, raw_wd, 320)
+        whole_passes("xd", E5M2, 0, raw_xd01, 320)
+        whole_passes("xd", E5M2, 2, raw_xd2, 320)
         V, S = nc.vector.tensor_copy, nc.scalar.copy
 
         def copy_shared(name, raw, width, c0, c1, share):
@@ -157,15 +156,25 @@ def tile_mix_jvp_tm_mul_kernel(tc, w, xd, wd, x, g, out):
         copy_shared("x2L", raw_x2L, HALF, 0, HALF, 128)
         product("x0", 0, (0, 1, 2, 3), 0, False)
         product("x2L", 2, (0, 1), 0, False)
-        copy_shared("x1", raw_x1, T, 0, HALF, 160)
-        copy_shared("x1", raw_x1, T, HALF, T, 128)
-        product("x1", 1, (0,), 0, True)
-        product("x1", 1, (1,), 0, True)
-        copy_shared("x2R", raw_x2R, HALF, 0, HALF, 128)
-        product("x1", 1, (2, 3), 0, False)
-        product("x2R", 2, (2,), HALF, True)
+        copy_shared("x1", raw_x1, T, 0, 128, 128)
+        copy_shared("x1", raw_x1, T, 128, 256, 0)
+        copy_shared("x1", raw_x1, T, 256, 384, 128)
+        copy_shared("x1", raw_x1, T, 384, 512, 0)
+        a0 = quantise("a0", grps["x1"], 0, 128, E4M3)
+        multiply("x", 1, 0, a0, 0, stop=True)
+        a1 = quantise("a1", grps["x1"], 128, 256, E4M3)
+        multiply("x", 1, 1, a1, 128, stop=True)
+        copy_shared("x2R", raw_x2R, HALF, 0, 64, 64)
+        copy_shared("x2R", raw_x2R, HALF, 64, 128, 0)
+        copy_shared("x2R", raw_x2R, HALF, 128, 256, 0)
+        aR = quantise("aR", grps["x1"], 256, 512, E4M3)
+        multiply("x", 1, 2, aR, 256, stop=False)
+        b2 = quantise("b2", grps["x2R"], 0, 128, E4M3)
+        multiply("x", 2, 2, b2, 256, stop=True)
+        multiply("x", 1, 3, aR, 256, stop=False)
         finish(0, 0, M)
-        product("x2R", 2, (3,), HALF, True)
+        b3 = quantise("b3", grps["x2R"], 128, 256, E4M3)
+        multiply("x", 2, 3, b3, 384, stop=True)
         finish(1, 0, M)
         finish(2, 0, M)
         finish(3, 0, M)

@@ -50,11 +50,10 @@ def tile_mix_jvp_tm_mul_kernel(tc, w, xd, wd, x, g, out):
             nc.sync.dma_start(out=r[:], in_=rows.rearrange("(p j) w -> p j w", j=PACK))
             return r[:]
 
-        def load_g(first, count):
-            gt = keep.tile([P, count, M], F32, name="g%d" % first, align_bytes=256)
-            rows = g[first * P : (first + count) * P, :]
-            nc.sync.dma_start(out=gt[:], in_=rows.rearrange("(i p) n -> p i n", p=P))
-            return [gt[:, i, :] for i in range(count)]
+        def load_g_columns(i, c0, c1):
+            gt = keep.tile([P, c1 - c0], F32, name="g%d_%d" % (i, c0), align_bytes=256)
+            nc.sync.dma_start(out=gt[:], in_=g[i * P : (i + 1) * P, c0:c1])
+            return gt[:]
 
         def grouped(name, width):
             return keep.tile([P, PACK * width], BF16, name="grp_%s" % name, align_bytes=64)
@@ -107,7 +106,7 @@ def tile_mix_jvp_tm_mul_kernel(tc, w, xd, wd, x, g, out):
         res = [keep.tile([P, M], F32, name="res%d" % i, align_bytes=256) for i in range(TILES)]
 
         def scale(i, c0, c1):
-            nc.vector.tensor_mul(out=res[i][:, c0:c1], in0=acc[i][:, c0:c1], in1=gs[i][:, c0:c1])
+            nc.vector.tensor_mul(out=res[i][:, c0:c1], in0=acc[i][:, c0:c1], in1=gs[i, c0])
 
         def store(i, c0, c1):
             nc.sync.dma_start(out=out[i * P : (i + 1) * P, c0:c1], in_=res[i][:, c0:c1])
@@ -117,64 +116,41 @@ def tile_mix_jvp_tm_mul_kernel(tc, w, xd, wd, x, g, out):
         raw_xd01 = load_passes("xd", xd, 0, 2)
         raw_xd2 = load_passes("xd", xd, 2, 1)
         raw_x0 = load_passes("x", x, 0, 1)
-        gs = []
-        raw_x2L = load_columns("x", x, 2, 0, HALF)
         raw_x1 = load_passes("x", x, 1, 1)[0]
+        raw_x2L = load_columns("x", x, 2, 0, HALF)
         raw_x2R = load_columns("x", x, 2, HALF, T)
-        gs = gs + load_g(0, 1)
-        gs = gs + load_g(1, 1)
-        gs = gs + load_g(2, 1)
-        gs = gs + load_g(3, 1)
+        g_pieces = [(0, 0, HALF), (0, HALF, M), (1, 0, M), (2, 0, M), (3, 0, M)]
+        gs = {(i, c0): load_g_columns(i, c0, c1) for i, c0, c1 in g_pieces}
 
         whole_passes("w", E4M3, 0, raw_w, 320)
         whole_passes("wd", E5M2, 0, raw_wd, 320)
         whole_passes("xd", E5M2, 0, raw_xd01, 320)
         whole_passes("xd", E5M2, 2, raw_xd2, 320)
-        V, S = nc.vector.tensor_copy, nc.scalar.copy
+        whole_passes("x", E4M3, 0, raw_x0, 320)
 
-        def copy_shared(name, raw, width, c0, c1, share):
-            if name not in grps:
-                grps[name] = grouped(name, width)
-            mid = c0 + share
-            if mid > c0:
-                round_and_interleave(V, grps[name], raw, c0, mid)
-            if mid < c1:
-                round_and_interleave(S, grps[name], raw, mid, c1)
+        def copy_shared(grp, raw, c0, mid, c1):
+            round_and_interleave(nc.vector.tensor_copy, grp, raw, c0, mid)
+            round_and_interleave(nc.scalar.copy, grp, raw, mid, c1)
 
-        def product(name, c, tiles, g0, stop):
-            c0, c1 = tiles[0] * P, (tiles[-1] + 1) * P
-            operand = quantise("%s_%d" % (name, c0), grps[name], c0 - g0, c1 - g0, E4M3)
-            for i in tiles:
-                multiply("x", c, i, operand, c0, stop=stop)
-
-        def finish(i, c0, c1):
-            scale(i, c0, c1)
-            store(i, c0, c1)
-
-        grps = {}
-        copy_shared("x0", raw_x0[0], T, 0, T, 320)
-        copy_shared("x2L", raw_x2L, HALF, 0, HALF, 128)
-        product("x0", 0, (0, 1, 2, 3), 0, False)
-        product("x2L", 2, (0, 1), 0, False)
-        copy_shared("x1", raw_x1, T, 0, 128, 128)
-        copy_shared("x1", raw_x1, T, 128, 256, 0)
-        copy_shared("x1", raw_x1, T, 256, 384, 128)
-        copy_shared("x1", raw_x1, T, 384, 512, 0)
-        a0 = quantise("a0", grps["x1"], 0, 128, E4M3)
-        multiply("x", 1, 0, a0, 0, stop=True)
-        a1 = quantise("a1", grps["x1"], 128, 256, E4M3)
-        multiply("x", 1, 1, a1, 128, stop=True)
-        copy_shared("x2R", raw_x2R, HALF, 0, 64, 64)
-        copy_shared("x2R", raw_x2R, HALF, 64, 128, 0)
-        copy_shared("x2R", raw_x2R, HALF, 128, 256, 0)
-        aR = quantise("aR", grps["x1"], 256, 512, E4M3)
-        multiply("x", 1, 2, aR, 256, stop=False)
-        b2 = quantise("b2", grps["x2R"], 0, 128, E4M3)
-        multiply("x", 2, 2, b2, 256, stop=True)
-        multiply("x", 1, 3, aR, 256, stop=False)
-        finish(0, 0, M)
-        b3 = quantise("b3", grps["x2R"], 128, 256, E4M3)
-        multiply("x", 2, 3, b3, 384, stop=True)
-        finish(1, 0, M)
-        finish(2, 0, M)
-        finish(3, 0, M)
+        x1, x2L, x2R = grouped("x1", T), grouped("x2L", HALF), grouped("x2R", HALF)
+        copy_shared(x1, raw_x1, 0, 128, 256)
+        copy_shared(x1, raw_x1, 256, 416, 512)
+        multiply("x", 1, 0, quantise("x1_0", x1, 0, 128, E4M3), 0)
+        multiply("x", 1, 1, quantise("x1_1", x1, 128, 256, E4M3), 128)
+        copy_shared(x2L, raw_x2L, 0, 64, 128)
+        copy_shared(x2L, raw_x2L, 128, 192, 256)
+        x1_right = quantise("x1_23", x1, 256, 512, E4M3)
+        multiply("x", 2, 0, quantise("x2_0", x2L, 0, 128, E4M3), 0, stop=True)
+        multiply("x", 2, 1, quantise("x2_1", x2L, 128, 256, E4M3), 128, stop=True)
+        multiply("x", 1, 2, x1_right, 256)
+        multiply("x", 1, 3, x1_right, 256)
+        copy_shared(x2R, raw_x2R, 0, 64, 128)
+        copy_shared(x2R, raw_x2R, 128, 192, 256)
+        scale(0, 0, HALF)
+        multiply("x", 2, 2, quantise("x2_2", x2R, 0, 128, E4M3), 256, stop=True)
+        scale(0, HALF, M)
+        store(0, 0, M)
+        multiply("x", 2, 3, quantise("x2_3", x2R, 128, 256, E4M3), 384, stop=True)
+        for i in range(1, TILES):
+            scale(i, 0, M)
+            store(i, 0, M)

@@ -119,14 +119,14 @@ def tile_mix_jvp_tm_mul_kernel(tc, w, xd, wd, x, g, out):
         raw_x1 = load_passes("x", x, 1, 1)[0]
         raw_x2L = load_columns("x", x, 2, 0, HALF)
         raw_x2R = load_columns("x", x, 2, HALF, T)
-        g_pieces = [(0, 0, HALF), (0, HALF, M), (1, 0, M), (2, 0, M), (3, 0, M)]
+        g_pieces = [(0, 0, M), (1, 0, M), (2, 0, M), (3, 0, M)]
         gs = {(i, c0): load_g_columns(i, c0, c1) for i, c0, c1 in g_pieces}
 
-        whole_passes("w", E4M3, 0, raw_w, 320)
-        whole_passes("wd", E5M2, 0, raw_wd, 320)
-        whole_passes("xd", E5M2, 0, raw_xd01, 320)
-        whole_passes("xd", E5M2, 2, raw_xd2, 320)
-        whole_passes("x", E4M3, 0, raw_x0, 320)
+        whole_passes("w", E4M3, 0, raw_w, 288)
+        whole_passes("wd", E5M2, 0, raw_wd, 288)
+        whole_passes("xd", E5M2, 0, raw_xd01, 288)
+        whole_passes("xd", E5M2, 2, raw_xd2, 288)
+        whole_passes("x", E4M3, 0, raw_x0, 288)
 
         def copy_shared(grp, raw, c0, mid, c1):
             round_and_interleave(nc.vector.tensor_copy, grp, raw, c0, mid)
@@ -134,21 +134,20 @@ def tile_mix_jvp_tm_mul_kernel(tc, w, xd, wd, x, g, out):
 
         x1, x2L, x2R = grouped("x1", T), grouped("x2L", HALF), grouped("x2R", HALF)
         copy_shared(x1, raw_x1, 0, 128, 256)
-        copy_shared(x1, raw_x1, 256, 416, 512)
+        copy_shared(x1, raw_x1, 256, 384, 512)
         multiply("x", 1, 0, quantise("x1_0", x1, 0, 128, E4M3), 0)
         multiply("x", 1, 1, quantise("x1_1", x1, 128, 256, E4M3), 128)
-        copy_shared(x2L, raw_x2L, 0, 64, 128)
-        copy_shared(x2L, raw_x2L, 128, 192, 256)
+        copy_shared(x2L, raw_x2L, 0, 96, 128)
+        round_and_interleave(nc.scalar.copy, x2L, raw_x2L, 128, 256)
         x1_right = quantise("x1_23", x1, 256, 512, E4M3)
         multiply("x", 2, 0, quantise("x2_0", x2L, 0, 128, E4M3), 0, stop=True)
         multiply("x", 2, 1, quantise("x2_1", x2L, 128, 256, E4M3), 128, stop=True)
         multiply("x", 1, 2, x1_right, 256)
         multiply("x", 1, 3, x1_right, 256)
         copy_shared(x2R, raw_x2R, 0, 64, 128)
-        copy_shared(x2R, raw_x2R, 128, 192, 256)
-        scale(0, 0, HALF)
+        round_and_interleave(nc.scalar.copy, x2R, raw_x2R, 128, 256)
         multiply("x", 2, 2, quantise("x2_2", x2R, 0, 128, E4M3), 256, stop=True)
-        scale(0, HALF, M)
+        scale(0, 0, M)
         store(0, 0, M)
         multiply("x", 2, 3, quantise("x2_3", x2R, 128, 256, E4M3), 384, stop=True)
         for i in range(1, TILES):

@@ -124,8 +124,7 @@ def tile_mix_jvp_tm_mul_kernel(tc, w, xd, wd, x, g, out):
 
         whole_passes("w", E4M3, 0, raw_w, 288)
         whole_passes("wd", E5M2, 0, raw_wd, 288)
-        whole_passes("xd", E5M2, 0, raw_xd01, 288)
-        whole_passes("xd", E5M2, 2, raw_xd2, 288)
+        whole_passes("xd", E5M2, 0, raw_xd01 + raw_xd2, 288)
         whole_passes("x", E4M3, 0, raw_x0, 288)
 
         def copy_shared(grp, raw, c0, mid, c1):
@@ -133,10 +132,11 @@ def tile_mix_jvp_tm_mul_kernel(tc, w, xd, wd, x, g, out):
             round_and_interleave(nc.scalar.copy, grp, raw, mid, c1)
 
         x1, x2L, x2R = grouped("x1", T), grouped("x2L", HALF), grouped("x2R", HALF)
-        copy_shared(x1, raw_x1, 0, 128, 256)
+        copy_shared(x1, raw_x1, 0, 160, 256)
         copy_shared(x1, raw_x1, 256, 384, 512)
-        multiply("x", 1, 0, quantise("x1_0", x1, 0, 128, E4M3), 0)
-        multiply("x", 1, 1, quantise("x1_1", x1, 128, 256, E4M3), 128)
+        x1_left = quantise("x1_01", x1, 0, 256, E4M3)
+        multiply("x", 1, 0, x1_left, 0)
+        multiply("x", 1, 1, x1_left, 0)
         copy_shared(x2L, raw_x2L, 0, 96, 128)
         round_and_interleave(nc.scalar.copy, x2L, raw_x2L, 128, 256)
         x1_right = quantise("x1_23", x1, 256, 512, E4M3)

@@ -111,29 +111,30 @@ def tile_mix_jvp_tm_mul_kernel(tc, w, xd, wd, x, g, out):
         def store(i, c0, c1):
             nc.sync.dma_start(out=out[i * P : (i + 1) * P, c0:c1], in_=res[i][:, c0:c1])
 
+
         raw_w = load_passes("w", w, 0, 3)
         raw_wd = load_passes("wd", wd, 0, 3)
         raw_xd01 = load_passes("xd", xd, 0, 2)
         raw_xd2 = load_passes("xd", xd, 2, 1)
         raw_x0 = load_passes("x", x, 0, 1)
         raw_x1 = load_passes("x", x, 1, 1)[0]
+        gs = {}
         raw_x2L = load_columns("x", x, 2, 0, HALF)
         raw_x2R = load_columns("x", x, 2, HALF, T)
-        g_pieces = [(0, 0, M), (1, 0, M), (2, 0, M), (3, 0, M)]
-        gs = {(i, c0): load_g_columns(i, c0, c1) for i, c0, c1 in g_pieces}
-
+        for i in range(4):
+            gs[i, 0] = load_g_columns(i, 0, M)
         whole_passes("w", E4M3, 0, raw_w, 288)
         whole_passes("wd", E5M2, 0, raw_wd, 288)
         whole_passes("xd", E5M2, 0, raw_xd01 + raw_xd2, 288)
         whole_passes("x", E4M3, 0, raw_x0, 288)
-
         def copy_shared(grp, raw, c0, mid, c1):
-            round_and_interleave(nc.vector.tensor_copy, grp, raw, c0, mid)
-            round_and_interleave(nc.scalar.copy, grp, raw, mid, c1)
-
+            if mid > c0:
+                round_and_interleave(nc.vector.tensor_copy, grp, raw, c0, mid)
+            if c1 > mid:
+                round_and_interleave(nc.scalar.copy, grp, raw, mid, c1)
         x1, x2L, x2R = grouped("x1", T), grouped("x2L", HALF), grouped("x2R", HALF)
         copy_shared(x1, raw_x1, 0, 160, 256)
-        copy_shared(x1, raw_x1, 256, 384, 512)
+        copy_shared(x1, raw_x1, 256, 256 + 128, 512)
         x1_left = quantise("x1_01", x1, 0, 256, E4M3)
         multiply("x", 1, 0, x1_left, 0)
         multiply("x", 1, 1, x1_left, 0)
@@ -141,11 +142,11 @@ def tile_mix_jvp_tm_mul_kernel(tc, w, xd, wd, x, g, out):
         round_and_interleave(nc.scalar.copy, x2L, raw_x2L, 128, 256)
         x1_right = quantise("x1_23", x1, 256, 512, E4M3)
         multiply("x", 2, 0, quantise("x2_0", x2L, 0, 128, E4M3), 0, stop=True)
-        multiply("x", 2, 1, quantise("x2_1", x2L, 128, 256, E4M3), 128, stop=True)
         multiply("x", 1, 2, x1_right, 256)
         multiply("x", 1, 3, x1_right, 256)
-        copy_shared(x2R, raw_x2R, 0, 64, 128)
+        copy_shared(x2R, raw_x2R, 0, 80, 128)
         round_and_interleave(nc.scalar.copy, x2R, raw_x2R, 128, 256)
+        multiply("x", 2, 1, quantise("x2_1", x2L, 128, 256, E4M3), 128, stop=True)
         multiply("x", 2, 2, quantise("x2_2", x2R, 0, 128, E4M3), 256, stop=True)
         scale(0, 0, M)
         store(0, 0, M)

@@ -112,7 +112,7 @@ def tile_mix_jvp_tm_mul_kernel(tc, w, xd, wd, x, g, out):
             nc.sync.dma_start(out=out[i * P : (i + 1) * P, c0:c1], in_=res[i][:, c0:c1])
 
 
-        raw_w = load_passes("w", w, 0, 3)
+        raw_w = load_passes("w", w, 0, 1) + load_passes("w", w, 1, 2)
         raw_wd = load_passes("wd", wd, 0, 3)
         raw_xd01 = load_passes("xd", xd, 0, 2)
         raw_xd2 = load_passes("xd", xd, 2, 1)

@@ -105,52 +105,114 @@ def tile_mix_jvp_tm_mul_kernel(tc, w, xd, wd, x, g, out):
 
         res = [keep.tile([P, M], F32, name="res%d" % i, align_bytes=256) for i in range(TILES)]
 
+        def g_view(i, c0, c1):
+            start = max(s for (t, s) in gs if t == i and s <= c0)
+            return gs[i, start][:, c0 - start : c1 - start]
+
         def scale(i, c0, c1):
-            nc.vector.tensor_mul(out=res[i][:, c0:c1], in0=acc[i][:, c0:c1], in1=gs[i, c0])
+            nc.vector.tensor_mul(out=res[i][:, c0:c1], in0=acc[i][:, c0:c1], in1=g_view(i, c0, c1))
 
         def store(i, c0, c1):
             nc.sync.dma_start(out=out[i * P : (i + 1) * P, c0:c1], in_=res[i][:, c0:c1])
 
 
-        raw_w = load_passes("w", w, 0, 1) + load_passes("w", w, 1, 2)
-        raw_wd = load_passes("wd", wd, 0, 3)
-        raw_xd01 = load_passes("xd", xd, 0, 2)
-        raw_xd2 = load_passes("xd", xd, 2, 1)
-        raw_x0 = load_passes("x", x, 0, 1)
-        raw_x1 = load_passes("x", x, 1, 1)[0]
-        gs = {}
-        raw_x2L = load_columns("x", x, 2, 0, HALF)
-        raw_x2R = load_columns("x", x, 2, HALF, T)
-        for i in range(4):
-            gs[i, 0] = load_g_columns(i, 0, M)
-        whole_passes("w", E4M3, 0, raw_w, 288)
-        whole_passes("wd", E5M2, 0, raw_wd, 288)
-        whole_passes("xd", E5M2, 0, raw_xd01 + raw_xd2, 288)
-        whole_passes("x", E4M3, 0, raw_x0, 288)
         def copy_shared(grp, raw, c0, mid, c1):
             if mid > c0:
                 round_and_interleave(nc.vector.tensor_copy, grp, raw, c0, mid)
             if c1 > mid:
                 round_and_interleave(nc.scalar.copy, grp, raw, mid, c1)
-        x1, x2L, x2R = grouped("x1", T), grouped("x2L", HALF), grouped("x2R", HALF)
-        copy_shared(x1, raw_x1, 0, 160, 256)
-        copy_shared(x1, raw_x1, 256, 256 + 128, 512)
-        x1_left = quantise("x1_01", x1, 0, 256, E4M3)
-        multiply("x", 1, 0, x1_left, 0)
-        multiply("x", 1, 1, x1_left, 0)
-        copy_shared(x2L, raw_x2L, 0, 96, 128)
-        round_and_interleave(nc.scalar.copy, x2L, raw_x2L, 128, 256)
-        x1_right = quantise("x1_23", x1, 256, 512, E4M3)
-        multiply("x", 2, 0, quantise("x2_0", x2L, 0, 128, E4M3), 0, stop=True)
-        multiply("x", 1, 2, x1_right, 256)
-        multiply("x", 1, 3, x1_right, 256)
-        copy_shared(x2R, raw_x2R, 0, 80, 128)
-        round_and_interleave(nc.scalar.copy, x2R, raw_x2R, 128, 256)
-        multiply("x", 2, 1, quantise("x2_1", x2L, 128, 256, E4M3), 128, stop=True)
-        multiply("x", 2, 2, quantise("x2_2", x2R, 0, 128, E4M3), 256, stop=True)
-        scale(0, 0, M)
-        store(0, 0, M)
-        multiply("x", 2, 3, quantise("x2_3", x2R, 128, 256, E4M3), 384, stop=True)
-        for i in range(1, TILES):
-            scale(i, 0, M)
-            store(i, 0, M)
+        FMT = {"w": E4M3, "x": E4M3, "wd": E5M2, "xd": E5M2}
+        grps = {}
+        def cp(name, c, share):
+            grps[name, c] = grouped("%s%d" % (name, c), T)
+            copy_shared(grps[name, c], raw[name, c], 0, share, T)
+        def qu(name, c):
+            operand = quantise("%s%d" % (name, c), grps[name, c], 0, T, FMT[name])
+            if name in ("w", "wd"):
+                moving[name, c] = operand
+            else:
+                for i in range(TILES):
+                    multiply(name, c, i, operand, 0, start=(name == "xd" and c == 0))
+        raw = {}
+        def ld(name, src, first, count):
+            for n, r in enumerate(load_passes(name, src, first, count)):
+                raw[name, first + n] = r
+        ld("w", w, 0, 1)
+        ld("w", w, 1, 1)
+        ld("w", w, 2, 1)
+        ld("wd", wd, 0, 1)
+        ld("wd", wd, 1, 1)
+        ld("wd", wd, 2, 1)
+        ld("xd", xd, 0, 1)
+        ld("xd", xd, 1, 1)
+        ld("xd", xd, 2, 1)
+        ld("x", x, 0, 1)
+        gs = {}
+        raw_1_0 = load_columns("x", x, 1, 0, 256)
+        raw_2_0 = load_columns("x", x, 2, 0, 256)
+        raw_1_2 = load_columns("x", x, 1, 256, 512)
+        gs[0, 0] = load_g_columns(0, 0, 512)
+        raw_2_2 = load_columns("x", x, 2, 256, 384)
+        raw_2_3 = load_columns("x", x, 2, 384, 512)
+        gs[1, 0] = load_g_columns(1, 0, 256)
+        gs[1, 256] = load_g_columns(1, 256, 512)
+        gs[2, 0] = load_g_columns(2, 0, 512)
+        gs[3, 0] = load_g_columns(3, 0, 512)
+
+        cp("w", 0, 288)
+        qu("w", 0)
+        cp("w", 1, 288)
+        qu("w", 1)
+        cp("w", 2, 288)
+        qu("w", 2)
+        cp("wd", 0, 288)
+        qu("wd", 0)
+        cp("wd", 1, 288)
+        qu("wd", 1)
+        cp("wd", 2, 288)
+        qu("wd", 2)
+        cp("xd", 0, 288)
+        qu("xd", 0)
+        cp("xd", 1, 288)
+        qu("xd", 1)
+        cp("xd", 2, 288)
+        qu("xd", 2)
+        cp("x", 0, 288)
+        xg = {1: grouped("x1", T), 2: grouped("x2", T)}
+        xq = {}
+        copy_shared(xg[1][:, PACK * 0 :], raw_1_0, 0, 96, 256)
+        qu("x", 0)
+        op = quantise("x1_0", xg[1], 0, 256, E4M3)
+        xq[1, 0] = (op, 0)
+        xq[1, 1] = (op, 0)
+        multiply("x", 1, 0, xq[1, 0][0], xq[1, 0][1], stop=False)
+        multiply("x", 1, 1, xq[1, 1][0], xq[1, 1][1], stop=False)
+        copy_shared(xg[2][:, PACK * 0 :], raw_2_0, 0, 112, 256)
+        op = quantise("x2_0", xg[2], 0, 256, E4M3)
+        xq[2, 0] = (op, 0)
+        xq[2, 1] = (op, 0)
+        multiply("x", 2, 0, xq[2, 0][0], xq[2, 0][1], stop=True)
+        multiply("x", 2, 1, xq[2, 1][0], xq[2, 1][1], stop=True)
+        copy_shared(xg[1][:, PACK * 256 :], raw_1_2, 0, 112, 256)
+        op = quantise("x1_2", xg[1], 256, 512, E4M3)
+        xq[1, 2] = (op, 256)
+        xq[1, 3] = (op, 256)
+        multiply("x", 1, 2, xq[1, 2][0], xq[1, 2][1], stop=False)
+        multiply("x", 1, 3, xq[1, 3][0], xq[1, 3][1], stop=False)
+        scale(0, 0, 512)
+        store(0, 0, 512)
+        copy_shared(xg[2][:, PACK * 256 :], raw_2_2, 0, 0, 128)
+        copy_shared(xg[2][:, PACK * 384 :], raw_2_3, 0, 48, 128)
+        op = quantise("x2_2", xg[2], 256, 384, E4M3)
+        xq[2, 2] = (op, 256)
+        multiply("x", 2, 2, xq[2, 2][0], xq[2, 2][1], stop=True)
+        scale(1, 0, 256)
+        op = quantise("x2_3", xg[2], 384, 512, E4M3)
+        xq[2, 3] = (op, 384)
+        multiply("x", 2, 3, xq[2, 3][0], xq[2, 3][1], stop=True)
+        scale(1, 256, 512)
+        store(1, 0, 512)
+        scale(2, 0, 512)
+        store(2, 0, 512)
+        scale(3, 0, 512)
+        store(3, 0, 512)

@@ -137,8 +137,7 @@ def tile_mix_jvp_tm_mul_kernel(tc, w, xd, wd, x, g, out):
         def ld(name, src, first, count):
             for n, r in enumerate(load_passes(name, src, first, count)):
                 raw[name, first + n] = r
-        ld("w", w, 0, 1)
-        ld("w", w, 1, 1)
+        ld("w", w, 0, 2)
         ld("w", w, 2, 1)
         ld("wd", wd, 0, 1)
         ld("wd", wd, 1, 1)
@@ -160,8 +159,8 @@ def tile_mix_jvp_tm_mul_kernel(tc, w, xd, wd, x, g, out):
         gs[3, 0] = load_g_columns(3, 0, 512)
 
         cp("w", 0, 288)
-        qu("w", 0)
         cp("w", 1, 288)
+        qu("w", 0)
         qu("w", 1)
         cp("w", 2, 288)
         qu("w", 2)
@@ -181,7 +180,11 @@ def tile_mix_jvp_tm_mul_kernel(tc, w, xd, wd, x, g, out):
         xg = {1: grouped("x1", T), 2: grouped("x2", T)}
         xq = {}
         copy_shared(xg[1][:, PACK * 0 :], raw_1_0, 0, 96, 256)
-        qu("x", 0)
+        op = quantise("x0", grps["x", 0], 0, T, E4M3)
+        for i in range(TILES):
+            xq[0, i] = (op, 0)
+        multiply("x", 0, 0, xq[0, 0][0], xq[0, 0][1], stop=False)
+        multiply("x", 0, 1, xq[0, 1][0], xq[0, 1][1], stop=False)
         op = quantise("x1_0", xg[1], 0, 256, E4M3)
         xq[1, 0] = (op, 0)
         xq[1, 1] = (op, 0)
@@ -193,6 +196,8 @@ def tile_mix_jvp_tm_mul_kernel(tc, w, xd, wd, x, g, out):
         xq[2, 1] = (op, 0)
         multiply("x", 2, 0, xq[2, 0][0], xq[2, 0][1], stop=True)
         multiply("x", 2, 1, xq[2, 1][0], xq[2, 1][1], stop=True)
+        multiply("x", 0, 2, xq[0, 2][0], xq[0, 2][1], stop=False)
+        multiply("x", 0, 3, xq[0, 3][0], xq[0, 3][1], stop=False)
         copy_shared(xg[1][:, PACK * 256 :], raw_1_2, 0, 112, 256)
         op = quantise("x1_2", xg[1], 256, 512, E4M3)
         xq[1, 2] = (op, 256)
@@ -202,16 +207,17 @@ def tile_mix_jvp_tm_mul_kernel(tc, w, xd, wd, x, g, out):
         scale(0, 0, 512)
         store(0, 0, 512)
         copy_shared(xg[2][:, PACK * 256 :], raw_2_2, 0, 0, 128)
-        copy_shared(xg[2][:, PACK * 384 :], raw_2_3, 0, 48, 128)
+        copy_shared(xg[2][:, PACK * 384 :], raw_2_3, 0, 32, 128)
         op = quantise("x2_2", xg[2], 256, 384, E4M3)
         xq[2, 2] = (op, 256)
         multiply("x", 2, 2, xq[2, 2][0], xq[2, 2][1], stop=True)
         scale(1, 0, 256)
+        store(1, 0, 256)
         op = quantise("x2_3", xg[2], 384, 512, E4M3)
         xq[2, 3] = (op, 384)
         multiply("x", 2, 3, xq[2, 3][0], xq[2, 3][1], stop=True)
         scale(1, 256, 512)
-        store(1, 0, 512)
+        store(1, 256, 512)
         scale(2, 0, 512)
         store(2, 0, 512)
         scale(3, 0, 512)

@@ -16,18 +16,20 @@ E5M2 = mybir.dt.float8_e5m2_x4
 P = 128
 PACK = 4
 K_PASS = P * PACK
-PASSES = K // K_PASS
 TILES = T // P
 HALF = T // 2
+FORMAT = {"w": E4M3, "x": E4M3, "wd": E5M2, "xd": E5M2}
+PARTNER = {"xd": "w", "x": "wd"}
 
 
-def round_and_interleave(copy, grp, raw, c0, c1, j0=0):
+def round_and_interleave(copy, grp, raw, c0, c1):
     dst = grp[:, PACK * c0 : PACK * c1].rearrange("p (c i j) -> p c j i", i=4, j=PACK)
-    copy(out=dst[:, :, j0 : j0 + raw.shape[1], :], in_=raw[:, :, c0:c1].rearrange("p j (c i) -> p c j i", i=4))
+    copy(out=dst, in_=raw[:, :, c0:c1].rearrange("p j (c i) -> p c j i", i=4))
 
 
 def tile_mix_jvp_tm_mul_kernel(tc, w, xd, wd, x, g, out):
     nc = tc.nc
+    source = {"w": w, "xd": xd, "wd": wd, "x": x}
 
     with ExitStack() as ctx:
         raws = ctx.enter_context(tc.tile_pool(name="raws", bufs=1))
@@ -35,190 +37,131 @@ def tile_mix_jvp_tm_mul_kernel(tc, w, xd, wd, x, g, out):
         psum = ctx.enter_context(tc.psum_pool(name="psum", bufs=1))
         ctx.enter_context(tc.manual_schedule())
 
-        def load_passes(name, src, first, count):
+        raw = {}
+        grouped = {}
+        quantised = {}
+        gs = {}
+        acc = [psum.tile([P, M], F32, name="acc%d" % i) for i in range(TILES)]
+        res = [keep.tile([P, M], F32, name="res%d" % i, align_bytes=256) for i in range(TILES)]
+
+        def load_passes(name, first, count, queue=nc.sync):
             r = raws.tile([P, count, PACK, T], F32, name="raw_%s%d" % (name, first), align_bytes=256)
-            rows = src[first * K_PASS : (first + count) * K_PASS, :]
-            nc.sync.dma_start(
+            rows = source[name][first * K_PASS : (first + count) * K_PASS, :]
+            queue.dma_start(
                 out=r[:].rearrange("p c j w -> p c (j w)"),
                 in_=rows.rearrange("(c p j) w -> p c (j w)", p=P, j=PACK),
             )
-            return [r[:, c, :, :] for c in range(count)]
+            for n in range(count):
+                raw[name, first + n, 0] = r[:, n, :, :]
 
-        def load_columns(name, src, c, c0, c1):
+        def load_columns(name, c, c0, c1):
             r = raws.tile([P, PACK, c1 - c0], F32, name="raw_%s%d_%d" % (name, c, c0), align_bytes=256)
-            rows = src[c * K_PASS : (c + 1) * K_PASS, c0:c1]
+            rows = source[name][c * K_PASS : (c + 1) * K_PASS, c0:c1]
             nc.sync.dma_start(out=r[:], in_=rows.rearrange("(p j) w -> p j w", j=PACK))
-            return r[:]
+            raw[name, c, c0] = r[:]
 
-        def load_g_columns(i, c0, c1):
+        def load_g(i, c0, c1):
             gt = keep.tile([P, c1 - c0], F32, name="g%d_%d" % (i, c0), align_bytes=256)
             nc.sync.dma_start(out=gt[:], in_=g[i * P : (i + 1) * P, c0:c1])
-            return gt[:]
+            gs[i, c0] = gt[:]
 
-        def grouped(name, width):
-            return keep.tile([P, PACK * width], BF16, name="grp_%s" % name, align_bytes=64)
+        def copy(name, c, c0, share):
+            if (name, c) not in grouped:
+                grouped[name, c] = keep.tile([P, PACK * T], BF16, name="grp_%s%d" % (name, c), align_bytes=64)
+            piece = raw[name, c, c0]
+            grp = grouped[name, c][:, PACK * c0 :]
+            width = piece.shape[2]
+            if share > 0:
+                round_and_interleave(nc.vector.tensor_copy, grp, piece, 0, share)
+            if share < width:
+                round_and_interleave(nc.scalar.copy, grp, piece, share, width)
 
-        acc = [psum.tile([P, M], F32, name="acc%d" % i) for i in range(TILES)]
-
-        def quantise(name, grp, c0, c1, fmt):
-            width = c1 - c0
-            cd = keep.tile([P, width], U32, name="codes_%s" % name, align_bytes=64)
-            sc = keep.tile([P, width], U8, name="scales_%s" % name, align_bytes=64)
-            nc.vector.quantize_mx(out=cd[:].bitcast(fmt), scales=sc[:], in_=grp[:, PACK * c0 : PACK * c1])
-            return cd, sc
-
-        moving = {}
-
-        def multiply(name, c, i, operand, c0, start=False, stop=False):
-            wname, lfmt, rfmt = ("w", E5M2, E4M3) if name == "xd" else ("wd", E4M3, E5M2)
-            cols = slice(i * P - c0, (i + 1) * P - c0)
-            nc.tensor.matmul_mx(
-                out=acc[i][:],
-                lhsT=operand[0][:, cols].bitcast(lfmt),
-                lhsT_scale=operand[1][:, cols],
-                rhs=moving[wname, c][0][:].bitcast(rfmt),
-                rhs_scale=moving[wname, c][1][:],
-                start=start,
-                stop=stop,
+        def quantise(name, c, c0, c1):
+            cd = keep.tile([P, c1 - c0], U32, name="codes_%s%d_%d" % (name, c, c0), align_bytes=64)
+            sc = keep.tile([P, c1 - c0], U8, name="scales_%s%d_%d" % (name, c, c0), align_bytes=64)
+            nc.vector.quantize_mx(
+                out=cd[:].bitcast(FORMAT[name]), scales=sc[:], in_=grouped[name, c][:, PACK * c0 : PACK * c1]
             )
+            quantised[name, c, c0] = (cd, sc)
 
-        def whole_passes(name, fmt, first, raw, split=HALF):
-            grps = []
-
-            def copy(n):
-                grp = grouped("%s%d" % (name, first + n), T)
-                round_and_interleave(nc.vector.tensor_copy, grp, raw[n], 0, split)
-                round_and_interleave(nc.scalar.copy, grp, raw[n], split, T)
-                grps.append(grp)
-
-            copy(0)
-            for n in range(len(raw)):
-                if n + 1 < len(raw):
-                    copy(n + 1)
-                c = first + n
-                operand = quantise("%s%d" % (name, c), grps[n], 0, T, fmt)
-                if name in ("w", "wd"):
-                    moving[name, c] = operand
-                else:
-                    for i in range(TILES):
-                        multiply(name, c, i, operand, 0, start=(name == "xd" and c == 0))
-
-        res = [keep.tile([P, M], F32, name="res%d" % i, align_bytes=256) for i in range(TILES)]
-
-        def g_view(i, c0, c1):
-            start = max(s for (t, s) in gs if t == i and s <= c0)
-            return gs[i, start][:, c0 - start : c1 - start]
+        def multiply(name, c, tiles, start=False, stop=False):
+            moving = quantised[PARTNER[name], c, 0]
+            for i in tiles:
+                c0 = max(s for (nm, cc, s) in quantised if nm == name and cc == c and s <= i * P)
+                cd, sc = quantised[name, c, c0]
+                cols = slice(i * P - c0, (i + 1) * P - c0)
+                nc.tensor.matmul_mx(
+                    out=acc[i][:],
+                    lhsT=cd[:, cols].bitcast(FORMAT[name]),
+                    lhsT_scale=sc[:, cols],
+                    rhs=moving[0][:].bitcast(FORMAT[PARTNER[name]]),
+                    rhs_scale=moving[1][:],
+                    start=start,
+                    stop=stop,
+                )
 
         def scale(i, c0, c1):
-            nc.vector.tensor_mul(out=res[i][:, c0:c1], in0=acc[i][:, c0:c1], in1=g_view(i, c0, c1))
+            first = max(s for (t, s) in gs if t == i and s <= c0)
+            nc.vector.tensor_mul(out=res[i][:, c0:c1], in0=acc[i][:, c0:c1], in1=gs[i, first][:, c0 - first : c1 - first])
 
-        def store(i, c0, c1):
-            nc.sync.dma_start(out=out[i * P : (i + 1) * P, c0:c1], in_=res[i][:, c0:c1])
+        def store(i, c0, c1, queue=nc.sync):
+            queue.dma_start(out=out[i * P : (i + 1) * P, c0:c1], in_=res[i][:, c0:c1])
 
+        load_passes("w", 0, 3)
+        load_passes("wd", 0, 2)
+        load_passes("wd", 2, 1)
+        for c in range(3):
+            load_passes("xd", c, 1)
+        load_passes("x", 0, 1)
+        load_columns("x", 1, 0, 256)
+        load_columns("x", 2, 0, 256)
+        load_columns("x", 1, 256, 512)
+        load_g(0, 0, 512)
+        load_columns("x", 2, 256, 384)
+        load_columns("x", 2, 384, 512)
+        load_g(1, 0, 256)
+        load_g(1, 256, 512)
+        load_g(2, 0, 512)
+        load_g(3, 0, 512)
 
-        def copy_shared(grp, raw, c0, mid, c1):
-            if mid > c0:
-                round_and_interleave(nc.vector.tensor_copy, grp, raw, c0, mid)
-            if c1 > mid:
-                round_and_interleave(nc.scalar.copy, grp, raw, mid, c1)
-        FMT = {"w": E4M3, "x": E4M3, "wd": E5M2, "xd": E5M2}
-        grps = {}
-        def cp(name, c, share):
-            grps[name, c] = grouped("%s%d" % (name, c), T)
-            copy_shared(grps[name, c], raw[name, c], 0, share, T)
-        def qu(name, c):
-            operand = quantise("%s%d" % (name, c), grps[name, c], 0, T, FMT[name])
-            if name in ("w", "wd"):
-                moving[name, c] = operand
-            else:
-                for i in range(TILES):
-                    multiply(name, c, i, operand, 0, start=(name == "xd" and c == 0))
-        raw = {}
-        def ld(name, src, first, count):
-            for n, r in enumerate(load_passes(name, src, first, count)):
-                raw[name, first + n] = r
-        ld("w", w, 0, 2)
-        ld("w", w, 2, 1)
-        ld("wd", wd, 0, 1)
-        ld("wd", wd, 1, 1)
-        ld("wd", wd, 2, 1)
-        ld("xd", xd, 0, 1)
-        ld("xd", xd, 1, 1)
-        ld("xd", xd, 2, 1)
-        ld("x", x, 0, 1)
-        gs = {}
-        raw_1_0 = load_columns("x", x, 1, 0, 256)
-        raw_2_0 = load_columns("x", x, 2, 0, 256)
-        raw_1_2 = load_columns("x", x, 1, 256, 512)
-        gs[0, 0] = load_g_columns(0, 0, 512)
-        raw_2_2 = load_columns("x", x, 2, 256, 384)
-        raw_2_3 = load_columns("x", x, 2, 384, 512)
-        gs[1, 0] = load_g_columns(1, 0, 256)
-        gs[1, 256] = load_g_columns(1, 256, 512)
-        gs[2, 0] = load_g_columns(2, 0, 512)
-        gs[3, 0] = load_g_columns(3, 0, 512)
-
-        cp("w", 0, 288)
-        cp("w", 1, 288)
-        qu("w", 0)
-        qu("w", 1)
-        cp("w", 2, 288)
-        qu("w", 2)
-        cp("wd", 0, 288)
-        qu("wd", 0)
-        cp("wd", 1, 288)
-        qu("wd", 1)
-        cp("wd", 2, 288)
-        qu("wd", 2)
-        cp("xd", 0, 288)
-        qu("xd", 0)
-        cp("xd", 1, 288)
-        qu("xd", 1)
-        cp("xd", 2, 288)
-        qu("xd", 2)
-        cp("x", 0, 288)
-        xg = {1: grouped("x1", T), 2: grouped("x2", T)}
-        xq = {}
-        copy_shared(xg[1][:, PACK * 0 :], raw_1_0, 0, 96, 256)
-        op = quantise("x0", grps["x", 0], 0, T, E4M3)
-        for i in range(TILES):
-            xq[0, i] = (op, 0)
-        multiply("x", 0, 0, xq[0, 0][0], xq[0, 0][1], stop=False)
-        multiply("x", 0, 1, xq[0, 1][0], xq[0, 1][1], stop=False)
-        op = quantise("x1_0", xg[1], 0, 256, E4M3)
-        xq[1, 0] = (op, 0)
-        xq[1, 1] = (op, 0)
-        multiply("x", 1, 0, xq[1, 0][0], xq[1, 0][1], stop=False)
-        multiply("x", 1, 1, xq[1, 1][0], xq[1, 1][1], stop=False)
-        copy_shared(xg[2][:, PACK * 0 :], raw_2_0, 0, 112, 256)
-        op = quantise("x2_0", xg[2], 0, 256, E4M3)
-        xq[2, 0] = (op, 0)
-        xq[2, 1] = (op, 0)
-        multiply("x", 2, 0, xq[2, 0][0], xq[2, 0][1], stop=True)
-        multiply("x", 2, 1, xq[2, 1][0], xq[2, 1][1], stop=True)
-        multiply("x", 0, 2, xq[0, 2][0], xq[0, 2][1], stop=False)
-        multiply("x", 0, 3, xq[0, 3][0], xq[0, 3][1], stop=False)
-        copy_shared(xg[1][:, PACK * 256 :], raw_1_2, 0, 112, 256)
-        op = quantise("x1_2", xg[1], 256, 512, E4M3)
-        xq[1, 2] = (op, 256)
-        xq[1, 3] = (op, 256)
-        multiply("x", 1, 2, xq[1, 2][0], xq[1, 2][1], stop=False)
-        multiply("x", 1, 3, xq[1, 3][0], xq[1, 3][1], stop=False)
+        for name in ("w", "wd"):
+            copy(name, 0, 0, 288)
+            copy(name, 1, 0, 288)
+            quantise(name, 0, 0, T)
+            copy(name, 2, 0, 288)
+            quantise(name, 1, 0, T)
+            quantise(name, 2, 0, T)
+        for c in range(3):
+            copy("xd", c, 0, 288)
+            quantise("xd", c, 0, T)
+            multiply("xd", c, range(TILES), start=(c == 0))
+        copy("x", 0, 0, 288)
+        copy("x", 1, 0, 96)
+        quantise("x", 0, 0, T)
+        multiply("x", 0, (0, 1))
+        quantise("x", 1, 0, 256)
+        multiply("x", 1, (0, 1))
+        copy("x", 2, 0, 112)
+        quantise("x", 2, 0, 256)
+        multiply("x", 2, (0, 1), stop=True)
+        multiply("x", 0, (2, 3))
+        copy("x", 1, 256, 112)
+        quantise("x", 1, 256, 512)
+        multiply("x", 1, (2, 3))
         scale(0, 0, 512)
         store(0, 0, 512)
-        copy_shared(xg[2][:, PACK * 256 :], raw_2_2, 0, 0, 128)
-        copy_shared(xg[2][:, PACK * 384 :], raw_2_3, 0, 32, 128)
-        op = quantise("x2_2", xg[2], 256, 384, E4M3)
-        xq[2, 2] = (op, 256)
-        multiply("x", 2, 2, xq[2, 2][0], xq[2, 2][1], stop=True)
+        copy("x", 2, 256, 0)
+        copy("x", 2, 384, 32)
+        quantise("x", 2, 256, 384)
+        multiply("x", 2, (2,), stop=True)
         scale(1, 0, 256)
-        store(1, 0, 256)
-        op = quantise("x2_3", xg[2], 384, 512, E4M3)
-        xq[2, 3] = (op, 384)
-        multiply("x", 2, 3, xq[2, 3][0], xq[2, 3][1], stop=True)
+        store(1, 0, 256, nc.scalar)
+        quantise("x", 2, 384, 512)
+        multiply("x", 2, (3,), stop=True)
         scale(1, 256, 512)
         store(1, 256, 512)
-        scale(2, 0, 512)
-        store(2, 0, 512)
-        scale(3, 0, 512)
-        store(3, 0, 512)
+        for i in (2, 3):
+            scale(i, 0, 256)
+            store(i, 0, 256, nc.scalar)
+            scale(i, 256, 512)
+            store(i, 256, 512)

@@ -155,13 +155,13 @@ def tile_mix_jvp_tm_mul_kernel(tc, w, xd, wd, x, g, out):
         quantise("x", 2, 256, 384)
         multiply("x", 2, (2,), stop=True)
         scale(1, 0, 256)
-        store(1, 0, 256, nc.scalar)
+        store(1, 0, 256)
         quantise("x", 2, 384, 512)
         multiply("x", 2, (3,), stop=True)
         scale(1, 256, 512)
         store(1, 256, 512)
         for i in (2, 3):
             scale(i, 0, 256)
-            store(i, 0, 256, nc.scalar)
+            store(i, 0, 256)
             scale(i, 256, 512)
             store(i, 256, 512)

@@ -41,7 +41,12 @@ def tile_mix_jvp_tm_mul_kernel(tc, w, xd, wd, x, g, out):
         grouped = {}
         quantised = {}
         gs = {}
-        acc = [psum.tile([P, M], F32, name="acc%d" % i) for i in range(TILES)]
+        width = {0: M, 1: M, 2: HALF, 3: HALF}
+        acc = {
+            (i, n0): psum.tile([P, width[i]], F32, name="acc%d_%d" % (i, n0))
+            for i in range(TILES)
+            for n0 in range(0, M, width[i])
+        }
         res = [keep.tile([P, M], F32, name="res%d" % i, align_bytes=256) for i in range(TILES)]
 
         def load_passes(name, first, count, queue=nc.sync):
@@ -64,6 +69,9 @@ def tile_mix_jvp_tm_mul_kernel(tc, w, xd, wd, x, g, out):
             gt = keep.tile([P, c1 - c0], F32, name="g%d_%d" % (i, c0), align_bytes=256)
             nc.sync.dma_start(out=gt[:], in_=g[i * P : (i + 1) * P, c0:c1])
             gs[i, c0] = gt[:]
+
+        def copy_part(copy_op, name, c, c0, a, b):
+            round_and_interleave(copy_op, grouped[name, c][:, PACK * c0 :], raw[name, c, c0], a, b)
 
         def copy(name, c, c0, share):
             if (name, c) not in grouped:
@@ -90,28 +98,30 @@ def tile_mix_jvp_tm_mul_kernel(tc, w, xd, wd, x, g, out):
                 c0 = max(s for (nm, cc, s) in quantised if nm == name and cc == c and s <= i * P)
                 cd, sc = quantised[name, c, c0]
                 cols = slice(i * P - c0, (i + 1) * P - c0)
-                nc.tensor.matmul_mx(
-                    out=acc[i][:],
-                    lhsT=cd[:, cols].bitcast(FORMAT[name]),
-                    lhsT_scale=sc[:, cols],
-                    rhs=moving[0][:].bitcast(FORMAT[PARTNER[name]]),
-                    rhs_scale=moving[1][:],
-                    start=start,
-                    stop=stop,
-                )
+                for n0 in range(0, M, width[i]):
+                    part = slice(n0, n0 + width[i])
+                    nc.tensor.matmul_mx(
+                        out=acc[i, n0][:],
+                        lhsT=cd[:, cols].bitcast(FORMAT[name]),
+                        lhsT_scale=sc[:, cols],
+                        rhs=moving[0][:, part].bitcast(FORMAT[PARTNER[name]]),
+                        rhs_scale=moving[1][:, part],
+                        start=start,
+                        stop=stop,
+                    )
 
         def scale(i, c0, c1):
             first = max(s for (t, s) in gs if t == i and s <= c0)
-            nc.vector.tensor_mul(out=res[i][:, c0:c1], in0=acc[i][:, c0:c1], in1=gs[i, first][:, c0 - first : c1 - first])
+            n0 = c0 - c0 % width[i]
+            nc.vector.tensor_mul(out=res[i][:, c0:c1], in0=acc[i, n0][:, c0 - n0 : c1 - n0], in1=gs[i, first][:, c0 - first : c1 - first])
 
         def store(i, c0, c1, queue=nc.sync):
             queue.dma_start(out=out[i * P : (i + 1) * P, c0:c1], in_=res[i][:, c0:c1])
 
         load_passes("w", 0, 3)
-        load_passes("wd", 0, 2)
-        load_passes("wd", 2, 1)
-        for c in range(3):
-            load_passes("xd", c, 1)
+        load_passes("wd", 0, 3)
+        load_passes("xd", 0, 2)
+        load_passes("xd", 2, 1)
         load_passes("x", 0, 1)
         load_columns("x", 1, 0, 256)
         load_columns("x", 2, 0, 256)
@@ -119,39 +129,45 @@ def tile_mix_jvp_tm_mul_kernel(tc, w, xd, wd, x, g, out):
         load_g(0, 0, 512)
         load_columns("x", 2, 256, 384)
         load_columns("x", 2, 384, 512)
-        load_g(1, 0, 256)
-        load_g(1, 256, 512)
-        load_g(2, 0, 512)
-        load_g(3, 0, 512)
-
+        for i in (1, 2, 3):
+            load_g(i, 0, 256)
+            load_g(i, 256, 512)
         for name in ("w", "wd"):
-            copy(name, 0, 0, 288)
-            copy(name, 1, 0, 288)
+            copy(name, 0, 0, 256)
+            copy(name, 1, 0, 256)
             quantise(name, 0, 0, T)
-            copy(name, 2, 0, 288)
+            copy(name, 2, 0, 256)
             quantise(name, 1, 0, T)
             quantise(name, 2, 0, T)
+        copy("xd", 0, 0, 256)
+        copy("xd", 1, 0, 256)
+        quantise("xd", 0, 0, 256)
+        quantise("xd", 0, 256, T)
+        quantise("xd", 1, 0, 256)
+        copy("xd", 2, 0, 256)
+        quantise("xd", 1, 256, T)
+        quantise("xd", 2, 0, 256)
+        quantise("xd", 2, 256, T)
         for c in range(3):
-            copy("xd", c, 0, 288)
-            quantise("xd", c, 0, T)
             multiply("xd", c, range(TILES), start=(c == 0))
-        copy("x", 0, 0, 288)
-        copy("x", 1, 0, 96)
-        quantise("x", 0, 0, T)
+        copy("x", 0, 0, 256)
+        quantise("x", 0, 0, 256)
         multiply("x", 0, (0, 1))
+        copy("x", 1, 0, 160)
+        quantise("x", 0, 256, T)
+        multiply("x", 0, (2, 3))
         quantise("x", 1, 0, 256)
         multiply("x", 1, (0, 1))
-        copy("x", 2, 0, 112)
+        copy("x", 2, 0, 160)
         quantise("x", 2, 0, 256)
         multiply("x", 2, (0, 1), stop=True)
-        multiply("x", 0, (2, 3))
-        copy("x", 1, 256, 112)
+        copy("x", 1, 256, 160)
         quantise("x", 1, 256, 512)
         multiply("x", 1, (2, 3))
         scale(0, 0, 512)
         store(0, 0, 512)
-        copy("x", 2, 256, 0)
-        copy("x", 2, 384, 32)
+        copy("x", 2, 256, 32)
+        copy("x", 2, 384, 64)
         quantise("x", 2, 256, 384)
         multiply("x", 2, (2,), stop=True)
         scale(1, 0, 256)

@@ -119,19 +119,21 @@ def tile_mix_jvp_tm_mul_kernel(tc, w, xd, wd, x, g, out):
             queue.dma_start(out=out[i * P : (i + 1) * P, c0:c1], in_=res[i][:, c0:c1])
 
         load_passes("w", 0, 3)
-        load_passes("wd", 0, 3)
-        load_passes("xd", 0, 2)
-        load_passes("xd", 2, 1)
+        load_passes("wd", 0, 2)
+        load_passes("wd", 2, 1)
+        for c in range(3):
+            load_passes("xd", c, 1)
         load_passes("x", 0, 1)
         load_columns("x", 1, 0, 256)
         load_columns("x", 2, 0, 256)
         load_columns("x", 1, 256, 512)
-        load_g(0, 0, 512)
         load_columns("x", 2, 256, 384)
+        load_g(0, 0, 512)
         load_columns("x", 2, 384, 512)
-        for i in (1, 2, 3):
-            load_g(i, 0, 256)
-            load_g(i, 256, 512)
+        load_g(1, 0, 256)
+        load_g(1, 256, 512)
+        load_g(2, 0, 512)
+        load_g(3, 0, 512)
         for name in ("w", "wd"):
             copy(name, 0, 0, 256)
             copy(name, 1, 0, 256)
@@ -139,37 +141,30 @@ def tile_mix_jvp_tm_mul_kernel(tc, w, xd, wd, x, g, out):
             copy(name, 2, 0, 256)
             quantise(name, 1, 0, T)
             quantise(name, 2, 0, T)
-        copy("xd", 0, 0, 256)
-        copy("xd", 1, 0, 256)
-        quantise("xd", 0, 0, 256)
-        quantise("xd", 0, 256, T)
-        quantise("xd", 1, 0, 256)
-        copy("xd", 2, 0, 256)
-        quantise("xd", 1, 256, T)
-        quantise("xd", 2, 0, 256)
-        quantise("xd", 2, 256, T)
         for c in range(3):
+            copy("xd", c, 0, 288)
+            quantise("xd", c, 0, T)
             multiply("xd", c, range(TILES), start=(c == 0))
         copy("x", 0, 0, 256)
         quantise("x", 0, 0, 256)
         multiply("x", 0, (0, 1))
-        copy("x", 1, 0, 160)
+        copy("x", 1, 0, 128)
         quantise("x", 0, 256, T)
         multiply("x", 0, (2, 3))
         quantise("x", 1, 0, 256)
         multiply("x", 1, (0, 1))
-        copy("x", 2, 0, 160)
+        copy("x", 2, 0, 128)
         quantise("x", 2, 0, 256)
         multiply("x", 2, (0, 1), stop=True)
-        copy("x", 1, 256, 160)
+        copy("x", 1, 256, 128)
         quantise("x", 1, 256, 512)
         multiply("x", 1, (2, 3))
+        copy("x", 2, 256, 0)
         scale(0, 0, 512)
         store(0, 0, 512)
-        copy("x", 2, 256, 32)
-        copy("x", 2, 384, 64)
         quantise("x", 2, 256, 384)
         multiply("x", 2, (2,), stop=True)
+        copy("x", 2, 384, 32)
         scale(1, 0, 256)
         store(1, 0, 256)
         quantise("x", 2, 384, 512)

@@ -16,15 +16,20 @@ E5M2 = mybir.dt.float8_e5m2_x4
 P = 128
 PACK = 4
 K_PASS = P * PACK
+PASSES = K // K_PASS
 TILES = T // P
 HALF = T // 2
 FORMAT = {"w": E4M3, "x": E4M3, "wd": E5M2, "xd": E5M2}
 PARTNER = {"xd": "w", "x": "wd"}
 
+SHARE_XD = 288
+SHARE_X1_RIGHT = 176
+SHARE_TILE3 = 32
 
-def round_and_interleave(copy, grp, raw, c0, c1):
+
+def round_and_interleave(copy_op, grp, raw, c0, c1):
     dst = grp[:, PACK * c0 : PACK * c1].rearrange("p (c i j) -> p c j i", i=4, j=PACK)
-    copy(out=dst, in_=raw[:, :, c0:c1].rearrange("p j (c i) -> p c j i", i=4))
+    copy_op(out=dst, in_=raw[:, :, c0:c1].rearrange("p j (c i) -> p c j i", i=4))
 
 
 def tile_mix_jvp_tm_mul_kernel(tc, w, xd, wd, x, g, out):
@@ -41,18 +46,13 @@ def tile_mix_jvp_tm_mul_kernel(tc, w, xd, wd, x, g, out):
         grouped = {}
         quantised = {}
         gs = {}
-        width = {0: M, 1: M, 2: HALF, 3: HALF}
-        acc = {
-            (i, n0): psum.tile([P, width[i]], F32, name="acc%d_%d" % (i, n0))
-            for i in range(TILES)
-            for n0 in range(0, M, width[i])
-        }
+        acc = [psum.tile([P, M], F32, name="acc%d" % i) for i in range(TILES)]
         res = [keep.tile([P, M], F32, name="res%d" % i, align_bytes=256) for i in range(TILES)]
 
-        def load_passes(name, first, count, queue=nc.sync):
+        def load_passes(name, first, count):
             r = raws.tile([P, count, PACK, T], F32, name="raw_%s%d" % (name, first), align_bytes=256)
             rows = source[name][first * K_PASS : (first + count) * K_PASS, :]
-            queue.dma_start(
+            nc.sync.dma_start(
                 out=r[:].rearrange("p c j w -> p c (j w)"),
                 in_=rows.rearrange("(c p j) w -> p c (j w)", p=P, j=PACK),
             )
@@ -70,19 +70,14 @@ def tile_mix_jvp_tm_mul_kernel(tc, w, xd, wd, x, g, out):
             nc.sync.dma_start(out=gt[:], in_=g[i * P : (i + 1) * P, c0:c1])
             gs[i, c0] = gt[:]
 
-        def copy_part(copy_op, name, c, c0, a, b):
-            round_and_interleave(copy_op, grouped[name, c][:, PACK * c0 :], raw[name, c, c0], a, b)
-
         def copy(name, c, c0, share):
             if (name, c) not in grouped:
                 grouped[name, c] = keep.tile([P, PACK * T], BF16, name="grp_%s%d" % (name, c), align_bytes=64)
             piece = raw[name, c, c0]
             grp = grouped[name, c][:, PACK * c0 :]
-            width = piece.shape[2]
             if share > 0:
                 round_and_interleave(nc.vector.tensor_copy, grp, piece, 0, share)
-            if share < width:
-                round_and_interleave(nc.scalar.copy, grp, piece, share, width)
+            round_and_interleave(nc.scalar.copy, grp, piece, share, piece.shape[2])
 
         def quantise(name, c, c0, c1):
             cd = keep.tile([P, c1 - c0], U32, name="codes_%s%d_%d" % (name, c, c0), align_bytes=64)
@@ -98,81 +93,80 @@ def tile_mix_jvp_tm_mul_kernel(tc, w, xd, wd, x, g, out):
                 c0 = max(s for (nm, cc, s) in quantised if nm == name and cc == c and s <= i * P)
                 cd, sc = quantised[name, c, c0]
                 cols = slice(i * P - c0, (i + 1) * P - c0)
-                for n0 in range(0, M, width[i]):
-                    part = slice(n0, n0 + width[i])
-                    nc.tensor.matmul_mx(
-                        out=acc[i, n0][:],
-                        lhsT=cd[:, cols].bitcast(FORMAT[name]),
-                        lhsT_scale=sc[:, cols],
-                        rhs=moving[0][:, part].bitcast(FORMAT[PARTNER[name]]),
-                        rhs_scale=moving[1][:, part],
-                        start=start,
-                        stop=stop,
-                    )
+                nc.tensor.matmul_mx(
+                    out=acc[i][:],
+                    lhsT=cd[:, cols].bitcast(FORMAT[name]),
+                    lhsT_scale=sc[:, cols],
+                    rhs=moving[0][:].bitcast(FORMAT[PARTNER[name]]),
+                    rhs_scale=moving[1][:],
+                    start=start,
+                    stop=stop,
+                )
 
-        def scale(i, c0, c1):
+        def scale_and_store(i, c0, c1):
             first = max(s for (t, s) in gs if t == i and s <= c0)
-            n0 = c0 - c0 % width[i]
-            nc.vector.tensor_mul(out=res[i][:, c0:c1], in0=acc[i, n0][:, c0 - n0 : c1 - n0], in1=gs[i, first][:, c0 - first : c1 - first])
+            nc.vector.tensor_mul(out=res[i][:, c0:c1], in0=acc[i][:, c0:c1], in1=gs[i, first][:, c0 - first : c1 - first])
+            nc.sync.dma_start(out=out[i * P : (i + 1) * P, c0:c1], in_=res[i][:, c0:c1])
 
-        def store(i, c0, c1, queue=nc.sync):
-            queue.dma_start(out=out[i * P : (i + 1) * P, c0:c1], in_=res[i][:, c0:c1])
-
-        load_passes("w", 0, 3)
+        load_passes("w", 0, PASSES)
         load_passes("wd", 0, 2)
         load_passes("wd", 2, 1)
-        for c in range(3):
+        for c in range(PASSES):
             load_passes("xd", c, 1)
         load_passes("x", 0, 1)
-        load_columns("x", 1, 0, 256)
-        load_columns("x", 2, 0, 256)
-        load_columns("x", 1, 256, 512)
-        load_columns("x", 2, 256, 384)
-        load_g(0, 0, 512)
-        load_columns("x", 2, 384, 512)
-        load_g(1, 0, 256)
-        load_g(1, 256, 512)
-        load_g(2, 0, 512)
-        load_g(3, 0, 512)
+        load_columns("x", 1, 0, HALF)
+        load_columns("x", 2, 0, HALF)
+        load_columns("x", 1, HALF, T)
+        load_columns("x", 2, 2 * P, 3 * P)
+        load_g(0, 0, M)
+        load_columns("x", 2, 3 * P, T)
+        load_g(1, 0, HALF)
+        load_g(1, HALF, M)
+        load_g(2, 0, M)
+        load_g(3, 0, M)
+
         for name in ("w", "wd"):
-            copy(name, 0, 0, 256)
-            copy(name, 1, 0, 256)
+            copy(name, 0, 0, HALF)
+            copy(name, 1, 0, HALF)
             quantise(name, 0, 0, T)
-            copy(name, 2, 0, 256)
+            copy(name, 2, 0, HALF)
             quantise(name, 1, 0, T)
             quantise(name, 2, 0, T)
-        for c in range(3):
-            copy("xd", c, 0, 288)
+
+        for c in range(PASSES):
+            copy("xd", c, 0, SHARE_XD)
             quantise("xd", c, 0, T)
             multiply("xd", c, range(TILES), start=(c == 0))
-        copy("x", 0, 0, 256)
-        quantise("x", 0, 0, 256)
+
+        copy("x", 0, 0, HALF)
+        quantise("x", 0, 0, HALF)
         multiply("x", 0, (0, 1))
-        copy("x", 1, 0, 128)
-        quantise("x", 0, 256, T)
+        copy("x", 1, 0, P)
+        quantise("x", 0, HALF, T)
+        quantise("x", 1, 0, P)
+        multiply("x", 1, (0,))
         multiply("x", 0, (2, 3))
-        quantise("x", 1, 0, 256)
-        multiply("x", 1, (0, 1))
-        copy("x", 2, 0, 128)
-        quantise("x", 2, 0, 256)
-        multiply("x", 2, (0, 1), stop=True)
-        copy("x", 1, 256, 128)
-        quantise("x", 1, 256, 512)
+        copy("x", 2, 0, P)
+        quantise("x", 1, P, HALF)
+        quantise("x", 2, 0, P)
+        multiply("x", 1, (1,))
+        multiply("x", 2, (0,), stop=True)
+        copy("x", 1, HALF, SHARE_X1_RIGHT)
+        quantise("x", 2, P, HALF)
+        multiply("x", 2, (1,), stop=True)
+
+        quantise("x", 1, HALF, T)
         multiply("x", 1, (2, 3))
-        copy("x", 2, 256, 0)
-        scale(0, 0, 512)
-        store(0, 0, 512)
-        quantise("x", 2, 256, 384)
+        copy("x", 2, 2 * P, 0)
+        scale_and_store(0, 0, M)
+        quantise("x", 2, 2 * P, 3 * P)
         multiply("x", 2, (2,), stop=True)
-        copy("x", 2, 384, 32)
-        scale(1, 0, 256)
-        store(1, 0, 256)
-        quantise("x", 2, 384, 512)
+        copy("x", 2, 3 * P, SHARE_TILE3)
+        scale_and_store(1, 0, HALF)
+        quantise("x", 2, 3 * P, T)
         multiply("x", 2, (3,), stop=True)
-        scale(1, 256, 512)
-        store(1, 256, 512)
+
+        scale_and_store(1, HALF, M)
         for i in (2, 3):
-            scale(i, 0, 256)
-            store(i, 0, 256)
-            scale(i, 256, 512)
-            store(i, 256, 512)
+            scale_and_store(i, 0, HALF)
+            scale_and_store(i, HALF, M)

from contextlib import ExitStack

import concourse.mybir as mybir

K, M, T = 1536, 512, 512

FLOPS = 2 * 2 * K * M * T

F32 = mybir.dt.float32
BF16 = mybir.dt.bfloat16
U32 = mybir.dt.uint32
U8 = mybir.dt.uint8
E4M3 = mybir.dt.float8_e4m3fn_x4
E5M2 = mybir.dt.float8_e5m2_x4

P = 128
PACK = 4
K_PASS = P * PACK
PASSES = K // K_PASS
TILES = T // P
HALF = T // 2
FORMAT = {"w": E4M3, "x": E4M3, "wd": E5M2, "xd": E5M2}
PARTNER = {"xd": "w", "x": "wd"}

SHARE_XD = 288
SHARE_X1_RIGHT = 176
SHARE_TILE3 = 32


def round_and_interleave(copy_op, grp, raw, c0, c1):
    dst = grp[:, PACK * c0 : PACK * c1].rearrange("p (c i j) -> p c j i", i=4, j=PACK)
    copy_op(out=dst, in_=raw[:, :, c0:c1].rearrange("p j (c i) -> p c j i", i=4))


def tile_mix_jvp_tm_mul_kernel(tc, w, xd, wd, x, g, out):
    nc = tc.nc
    source = {"w": w, "xd": xd, "wd": wd, "x": x}

    with ExitStack() as ctx:
        raws = ctx.enter_context(tc.tile_pool(name="raws", bufs=1))
        keep = ctx.enter_context(tc.tile_pool(name="keep", bufs=1))
        psum = ctx.enter_context(tc.psum_pool(name="psum", bufs=1))
        ctx.enter_context(tc.manual_schedule())

        raw = {}
        grouped = {}
        quantised = {}
        gs = {}
        acc = [psum.tile([P, M], F32, name="acc%d" % i) for i in range(TILES)]
        res = [keep.tile([P, M], F32, name="res%d" % i, align_bytes=256) for i in range(TILES)]

        def load_passes(name, first, count):
            r = raws.tile([P, count, PACK, T], F32, name="raw_%s%d" % (name, first), align_bytes=256)
            rows = source[name][first * K_PASS : (first + count) * K_PASS, :]
            nc.sync.dma_start(
                out=r[:].rearrange("p c j w -> p c (j w)"),
                in_=rows.rearrange("(c p j) w -> p c (j w)", p=P, j=PACK),
            )
            for n in range(count):
                raw[name, first + n, 0] = r[:, n, :, :]

        def load_columns(name, c, c0, c1):
            r = raws.tile([P, PACK, c1 - c0], F32, name="raw_%s%d_%d" % (name, c, c0), align_bytes=256)
            rows = source[name][c * K_PASS : (c + 1) * K_PASS, c0:c1]
            nc.sync.dma_start(out=r[:], in_=rows.rearrange("(p j) w -> p j w", j=PACK))
            raw[name, c, c0] = r[:]

        def load_g(i, c0, c1):
            gt = keep.tile([P, c1 - c0], F32, name="g%d_%d" % (i, c0), align_bytes=256)
            nc.sync.dma_start(out=gt[:], in_=g[i * P : (i + 1) * P, c0:c1])
            gs[i, c0] = gt[:]

        def copy(name, c, c0, share):
            if (name, c) not in grouped:
                grouped[name, c] = keep.tile([P, PACK * T], BF16, name="grp_%s%d" % (name, c), align_bytes=64)
            piece = raw[name, c, c0]
            grp = grouped[name, c][:, PACK * c0 :]
            if share > 0:
                round_and_interleave(nc.vector.tensor_copy, grp, piece, 0, share)
            round_and_interleave(nc.scalar.copy, grp, piece, share, piece.shape[2])

        def quantise(name, c, c0, c1):
            cd = keep.tile([P, c1 - c0], U32, name="codes_%s%d_%d" % (name, c, c0), align_bytes=64)
            sc = keep.tile([P, c1 - c0], U8, name="scales_%s%d_%d" % (name, c, c0), align_bytes=64)
            nc.vector.quantize_mx(
                out=cd[:].bitcast(FORMAT[name]), scales=sc[:], in_=grouped[name, c][:, PACK * c0 : PACK * c1]
            )
            quantised[name, c, c0] = (cd, sc)

        def multiply(name, c, tiles, start=False, stop=False):
            moving = quantised[PARTNER[name], c, 0]
            for i in tiles:
                c0 = max(s for (nm, cc, s) in quantised if nm == name and cc == c and s <= i * P)
                cd, sc = quantised[name, c, c0]
                cols = slice(i * P - c0, (i + 1) * P - c0)
                nc.tensor.matmul_mx(
                    out=acc[i][:],
                    lhsT=cd[:, cols].bitcast(FORMAT[name]),
                    lhsT_scale=sc[:, cols],
                    rhs=moving[0][:].bitcast(FORMAT[PARTNER[name]]),
                    rhs_scale=moving[1][:],
                    start=start,
                    stop=stop,
                )

        def scale_and_store(i, c0, c1):
            first = max(s for (t, s) in gs if t == i and s <= c0)
            nc.vector.tensor_mul(out=res[i][:, c0:c1], in0=acc[i][:, c0:c1], in1=gs[i, first][:, c0 - first : c1 - first])
            nc.sync.dma_start(out=out[i * P : (i + 1) * P, c0:c1], in_=res[i][:, c0:c1])

        load_passes("w", 0, PASSES)
        load_passes("wd", 0, 2)
        load_passes("wd", 2, 1)
        for c in range(PASSES):
            load_passes("xd", c, 1)
        load_passes("x", 0, 1)
        load_columns("x", 1, 0, HALF)
        load_columns("x", 2, 0, HALF)
        load_columns("x", 1, HALF, T)
        load_columns("x", 2, 2 * P, 3 * P)
        load_g(0, 0, M)
        load_columns("x", 2, 3 * P, T)
        load_g(1, 0, HALF)
        load_g(1, HALF, M)
        load_g(2, 0, M)
        load_g(3, 0, M)

        for name in ("w", "wd"):
            copy(name, 0, 0, HALF)
            copy(name, 1, 0, HALF)
            quantise(name, 0, 0, T)
            copy(name, 2, 0, HALF)
            quantise(name, 1, 0, T)
            quantise(name, 2, 0, T)

        for c in range(PASSES):
            copy("xd", c, 0, SHARE_XD)
            quantise("xd", c, 0, T)
            multiply("xd", c, range(TILES), start=(c == 0))

        copy("x", 0, 0, HALF)
        quantise("x", 0, 0, HALF)
        multiply("x", 0, (0, 1))
        copy("x", 1, 0, P)
        quantise("x", 0, HALF, T)
        quantise("x", 1, 0, P)
        multiply("x", 1, (0,))
        multiply("x", 0, (2, 3))
        copy("x", 2, 0, P)
        quantise("x", 1, P, HALF)
        quantise("x", 2, 0, P)
        multiply("x", 1, (1,))
        multiply("x", 2, (0,), stop=True)
        copy("x", 1, HALF, SHARE_X1_RIGHT)
        quantise("x", 2, P, HALF)
        multiply("x", 2, (1,), stop=True)

        quantise("x", 1, HALF, T)
        multiply("x", 1, (2, 3))
        copy("x", 2, 2 * P, 0)
        scale_and_store(0, 0, M)
        quantise("x", 2, 2 * P, 3 * P)
        multiply("x", 2, (2,), stop=True)
        copy("x", 2, 3 * P, SHARE_TILE3)
        scale_and_store(1, 0, HALF)
        quantise("x", 2, 3 * P, T)
        multiply("x", 2, (3,), stop=True)

        scale_and_store(1, HALF, M)
        for i in (2, 3):
            scale_and_store(i, 0, HALF)
            scale_and_store(i, HALF, M)
